import numpy as np
import ml_dtypes


def mxq(x, axis, fmt="e4m3"):
    dtype, down = {"e4m3": (ml_dtypes.float8_e4m3fn, 7), "e5m2": (ml_dtypes.float8_e5m2, 14)}[fmt]
    v = np.moveaxis(np.asarray(x, np.float32).astype(ml_dtypes.bfloat16).astype(np.float64), axis, -1)
    blocks = v.reshape(v.shape[:-1] + (-1, 32))
    amax = np.abs(blocks).max(-1, keepdims=True)
    byte = np.maximum(np.where(amax > 0, np.frexp(amax)[1] - 1 + 127, 0) - down, 1)
    scale = np.exp2(byte - 127.0)
    codes = (blocks / scale).astype(np.float32).astype(dtype).astype(np.float64)
    return np.moveaxis((codes * scale).reshape(v.shape), -1, axis)


WIDE = False


def mx_kscale(k):
    if not WIDE:
        return np.ones(k)
    levels = np.array([10, -10, 5, -5, 0])
    if k % 512:
        return np.exp2(np.random.permutation(np.resize(levels, k // 32))).repeat(32)
    a = np.empty((k // 512, 16))
    for p in range(k // 512):
        a[p, :8] = np.random.permutation(np.resize(levels, 8))
        for g in range(8):
            far = levels[np.abs(levels - a[p, g]) >= 10]
            a[p, g + 8] = far[np.random.randint(len(far))]
    return np.exp2(a.ravel()).repeat(32)


def f64(x):
    return np.asarray(x).astype(np.float64)


def striped(idx):
    return np.tile(idx.reshape(-1, 16).T, (8, 1)).astype(np.uint16)


def unstriped(offs):
    return offs[:16].T.reshape(-1).astype(np.int64)


E2M1 = np.array([0.0, 0.5, 1.0, 1.5, 2.0, 3.0, 4.0, 6.0, -0.0, -0.5, -1.0, -1.5, -2.0, -3.0, -4.0, -6.0])


def pack_weight(w, fmt):
    k, n = w.shape
    w = f64(np.asarray(w, np.float32).astype(ml_dtypes.bfloat16)).reshape(k // 32, 32, n)
    amax = np.abs(w).max(1)
    if fmt == "e4m3":
        byte = np.frexp(amax)[1] - 1 + 127 - 7
    else:
        mant, ex = np.frexp(amax / 6.0)
        byte = np.where(mant > 0.5, ex, ex - 1) + 127
    byte = np.clip(np.where(amax > 0, byte, 1), 1, 254)
    scaled = (w * np.exp2(127.0 - byte)[:, None, :]).reshape(k, n).astype(np.float32)
    by_word = np.ascontiguousarray(scaled.reshape(k // 512, 128, 4, n).transpose(0, 1, 3, 2))
    if fmt == "e4m3":
        words = by_word.astype(ml_dtypes.float8_e4m3fn).view(np.uint8)
    else:
        c = by_word.astype(ml_dtypes.float4_e2m1fn).view(np.uint8) & 0xF
        words = (c[..., 0::2] | (c[..., 1::2] << 4)).reshape(k // 512, 128, 2 * n)
    return np.ascontiguousarray(words), np.ascontiguousarray(byte.astype(np.uint8).reshape(k // 512, 16, n))


def unpack_weight(words, scales, fmt):
    g, _, n = scales.shape
    words = np.ascontiguousarray(words).reshape(g, 128, n, -1)
    if fmt == "e4m3":
        vals = words.view(ml_dtypes.float8_e4m3fn).astype(np.float64)
    else:
        nib = np.empty((g, 128, n, 4), np.uint8)
        nib[..., 0::2] = words & 0xF
        nib[..., 1::2] = words >> 4
        vals = E2M1[nib]
    vals = vals * np.repeat(np.exp2(scales.astype(np.float64) - 127.0), 8, axis=1)[..., None]
    return vals.transpose(0, 1, 3, 2).reshape(g * 512, n)


def gelu(v):
    return 0.5 * v * (1.0 + np.tanh(np.sqrt(2.0 / np.pi) * (v + 0.044715 * v**3)))


def striped8(idx):
    return np.concatenate([v.reshape(-1, 16).T for v in idx]).astype(np.uint16)


def unstriped8(offs):
    return np.stack([offs[16 * g:16 * g + 16].T.reshape(-1) for g in range(8)]).astype(np.int64)


def heads(h, wgt, idx8):
    r = np.arange(h.shape[0])
    return wgt[r // 4 % 128] * h[r[:, None], idx8[r % 512 // 64]]


K, T, S, P, H, N = 512, 4096, 2048, 1024, 1024, 512

def setup_inputs():
    n = np.random.standard_normal
    s = mx_kscale(K)[:, None]
    u = mx_kscale(H)[:, None]
    tab_words, tab_scales = pack_weight(n((K, T)) * s, "e4m3")
    w4_words, w4_scales = pack_weight(n((K, H)) / np.sqrt(K) / s, "e2m1")
    return {
        "tab_words": tab_words, "tab_scales": tab_scales,
        "offs": striped(np.random.permutation(T)[:S]),
        "w4_words": w4_words, "w4_scales": w4_scales,
        "gain": (np.exp(0.3 * n(H)) * u[:, 0]).astype(np.float32),
        "offs2": striped8(np.stack([np.random.permutation(S)[:P] for _ in range(8)])),
        "wgt": np.repeat(np.random.uniform(0.5, 2.0, (8, P)), 16, axis=0).astype(np.float32),
        "budget": (np.exp(0.5 * n((H, P))) * u).astype(np.float32),
        "w2": (n((H, N)) / np.sqrt(H) / u).astype(np.float32),
        "best": n((N, P)).astype(np.float32),
    }

def reference(tab_words, tab_scales, offs, w4_words, w4_scales, gain, offs2, wgt, budget, w2, best):
    v = unpack_weight(tab_words, tab_scales, "e4m3")[:, unstriped(offs)]
    a = unpack_weight(w4_words, w4_scales, "e2m1").T @ v
    h = f64(gain)[:, None] * np.log(1.0 + np.exp(a))
    x = heads(h, f64(wgt), unstriped8(offs2))
    z = np.minimum(x, f64(budget))
    y = mxq(f64(w2), 0, "e4m3").T @ mxq(z, 0, "e4m3")
    return y - f64(best)

@@ -1,0 +1,200 @@
+from contextlib import ExitStack
+
+import concourse.mybir as mybir
+
+K, T, S, M, H, N = 512, 4096, 2048, 1024, 1024, 512
+FLOPS = 2 * K * H * S + 2 * H * N * M
+
+F32 = mybir.dt.float32
+BF16 = mybir.dt.bfloat16
+I32 = mybir.dt.int32
+U32 = mybir.dt.uint32
+U16 = mybir.dt.uint16
+U8 = mybir.dt.uint8
+FP8X4 = mybir.dt.float8_e4m3fn_x4
+FP4X4 = mybir.dt.float4_e2m1fn_x4
+ALU = mybir.AluOpType
+ACT = mybir.ActivationFunctionType
+
+P = 128
+BANK = 512
+CHUNKS = S // BANK
+TILES = H // P
+FIRST = 6
+
+
+def tile_list_eclass_cost_extraction_kernel(
+    tc, tab_words, tab_scales, offs, w4_words, w4_scales, gain, offs2, wgt, budget, w2, best, out
+):
+    nc = tc.nc
+    with ExitStack() as ctx:
+        keep = ctx.enter_context(tc.tile_pool(name="keep", bufs=1))
+        psum = ctx.enter_context(tc.psum_pool(name="psum", bufs=8))
+
+        idx = keep.tile([P, S // 16], U16, name="idx")
+        nc.sync.dma_start(idx[:], offs)
+        w4raw = keep.tile([P, 2 * H], U8, name="w4raw", tag="slot_b")
+        nc.sync.dma_start(w4raw[:].bitcast(I32), w4_words[0].bitcast(I32))
+        tabw = keep.tile([P, T], I32, name="tabw")
+        nc.sync.dma_start(tabw[:], tab_words[0].rearrange("p t i -> p (t i)").bitcast(I32))
+
+        tabs = keep.tile([P, T], U8, name="tabs")
+        nc.vector.memset(tabs[:].bitcast(I32), 0)
+        w4sraw = keep.tile([P, H], U8, name="w4sraw", tag="slot_a")
+        nc.gpsimd.memset(w4sraw[:].bitcast(I32), 0)
+        for q in range(4):
+            nc.scalar.dma_start(tabs[32 * q : 32 * q + 4, :].bitcast(I32), tab_scales[0, 4 * q : 4 * q + 4, :].bitcast(I32))
+        for q in range(4):
+            (nc.gpsimd if q < 2 else nc.scalar).dma_start(w4sraw[32 * q : 32 * q + 4, :].bitcast(I32), w4_scales[0, 4 * q : 4 * q + 4, :].bitcast(I32))
+        gain_sb = keep.tile([P, 2, 4], F32, name="gain_sb")
+        nc.gpsimd.dma_start(gain_sb[:], gain.rearrange("(b p i) -> p b i", b=2, i=4))
+        idx2 = keep.tile([P, M // 16], U16, name="idx2")
+        nc.sync.dma_start(idx2[:], offs2)
+
+        w4w = keep.tile([P, 2 * H], U8, name="w4w", align_bytes=64)
+        w4s = keep.tile([P, H], U8, name="w4s", align_bytes=64)
+        nc.vector.tensor_copy(
+            w4w[:].bitcast(U16).rearrange("p (b t m) -> p b t m", b=2, t=4),
+            w4raw[:].bitcast(U16).rearrange("p (b m t) -> p b t m", b=2, t=4),
+        )
+        nc.vector.tensor_copy(
+            w4s[:].rearrange("p (b t m) -> p b t m", b=2, t=4),
+            w4sraw[:].rearrange("p (b m t) -> p b t m", b=2, t=4),
+        )
+        wgt_sb = keep.tile([P, M], F32, name="wgt_sb", tag="slot_b")
+        nc.sync.dma_start(wgt_sb[:], wgt)
+        w2raw = keep.tile([P, 2, 4, N], F32, name="w2raw", tag="slot_a")
+        nc.sync.dma_start(w2raw[:], w2.rearrange("(b p j) n -> p b j n", b=2, j=4))
+
+        vw, vs = [], []
+        h = {}
+
+        def raw_cost(k, c):
+            acc = psum.tile([P, BANK], F32, name="acc", tag="bank")
+            nc.tensor.matmul_mx(
+                out=acc[:],
+                lhsT=w4w[:, 2 * P * k : 2 * P * (k + 1)].bitcast(FP4X4),
+                lhsT_scale=w4s[:, P * k : P * (k + 1)],
+                rhs=vw[c][:].bitcast(FP8X4),
+                rhs_scale=vs[c][:],
+                start=True,
+                stop=True,
+            )
+            nc.scalar.activation(h[k][:, BANK * c : BANK * (c + 1)], acc[:], ACT.Exp)
+
+        for k in range(FIRST):
+            h[k] = keep.tile([P, S], F32, name="h%d" % k, tag="h%d" % k)
+        for c in range(CHUNKS):
+            cols = idx[:, 32 * c : 32 * (c + 1)]
+            vs.append(keep.tile([P, BANK], U8, name="vs%d" % c, align_bytes=64))
+            vw.append(keep.tile([P, BANK], U32, name="vw%d" % c, align_bytes=64))
+            nc.vector.tensor_copy(vs[c][:], tabs[:].indirect(cols))
+            nc.vector.tensor_copy(vw[c][:], tabw[:].bitcast(U32).indirect(cols))
+            for k in range(FIRST):
+                raw_cost(k, c)
+
+        w2bf = keep.tile([P, 2, N * 4], BF16, name="w2bf", tag="grouped", align_bytes=64)
+        w2w = keep.tile([P, 2 * N], U32, name="w2w", align_bytes=64)
+        w2s = keep.tile([P, 2 * N], U8, name="w2s", align_bytes=64)
+        for b in range(2):
+            nc.vector.tensor_copy(
+                w2bf[:, b, :].rearrange("p (c i t) -> p c t i", i=4, t=4),
+                w2raw[:, b, :, :].rearrange("p t (c i) -> p c t i", i=4),
+            )
+        wg = []
+        for k in range(TILES):
+            wg.append(keep.tile([P, M], F32, name="wg%d" % k, tag="wg%d" % k))
+            nc.vector.tensor_scalar(wg[k][:], wgt_sb[:], gain_sb[:, k // 4, k % 4 : k % 4 + 1], None, ALU.mult)
+        nc.vector.quantize_mx(out=w2w[:].bitcast(FP8X4), scales=w2s[:], in_=w2bf[:].rearrange("p b c -> p (b c)"))
+
+        bud = []
+        for b in range(2):
+            bud.append(keep.tile([P, 4, M], F32, name="bud%d" % b, tag=("slot_a", "slot_b")[b]))
+            nc.sync.dma_start(bud[b][:], budget[512 * b : 512 * (b + 1), :].rearrange("(p i) m -> p i m", i=4))
+        res = []
+        x = [keep.tile([P, 4, M], F32, name="x0"), keep.tile([P, 4, M], F32, name="x1")]
+        z = {}
+        zw, zs = {}, {}
+        zall = keep.tile([P, 2, BANK * 4], BF16, name="zall", tag="grouped", align_bytes=64)
+        for u in range(2):
+            z[0, u] = zall[:, u, :]
+            z[1, u] = keep.tile([P, BANK * 4], BF16, name="z1%d" % u, align_bytes=64)[:]
+            for b in range(2):
+                zw[b, u] = keep.tile([P, BANK], U32, name="zw%d%d" % (b, u), align_bytes=64)
+                zs[b, u] = keep.tile([P, BANK], U8, name="zs%d%d" % (b, u), align_bytes=64)
+
+        def softplus(k):
+            nc.scalar.activation(h[k][:], h[k][:], ACT.Ln, bias=1.0)
+
+        def pick(k, m0, m1):
+            nc.vector.tensor_tensor(
+                x[k // 4][:, k % 4, m0:m1], h[k][:].indirect(idx2[:, m0 // 16 : m1 // 16]), wg[k][:, m0:m1], ALU.mult
+            )
+
+        def cap(b, u):
+            nc.vector.tensor_tensor(
+                z[b, u].rearrange("p (c i t) -> p c t i", i=4, t=4),
+                x[b][:, :, BANK * u : BANK * (u + 1)].rearrange("p t (c i) -> p c t i", i=4),
+                bud[b][:, :, BANK * u : BANK * (u + 1)].rearrange("p t (c i) -> p c t i", i=4),
+                ALU.min,
+            )
+
+        def quant(b, u):
+            nc.vector.quantize_mx(out=zw[b, u][:].bitcast(FP8X4), scales=zs[b, u][:], in_=z[b, u])
+
+        y = {}
+
+        def readout(b, u):
+            for t in range(4):
+                if b == 0:
+                    y[u, t] = psum.tile([P, BANK], F32, name="y", tag="bank")
+                cols = slice(N * b + P * t, N * b + P * (t + 1))
+                nc.tensor.matmul_mx(
+                    out=y[u, t][:],
+                    lhsT=w2w[:, cols].bitcast(FP8X4),
+                    lhsT_scale=w2s[:, cols],
+                    rhs=zw[b, u][:].bitcast(FP8X4),
+                    rhs_scale=zs[b, u][:],
+                    start=(b == 0),
+                    stop=(b == 1),
+                )
+
+        def finish(u, t):
+            nc.vector.tensor_tensor(res[u][:, t, :], y[u, t][:], res[u][:, t, :], ALU.subtract)
+            nc.sync.dma_start(out[P * t : P * (t + 1), BANK * u : BANK * (u + 1)], res[u][:, t, :])
+
+        for k in range(FIRST):
+            softplus(k)
+            pick(k, 0, M)
+            if k < 2:
+                res.append(keep.tile([P, 4, BANK], F32, name="res%d" % k, tag="wg%d" % k))
+                nc.sync.dma_start(res[k][:], best[:, BANK * k : BANK * (k + 1)].rearrange("(t p) m -> p t m", p=P))
+            if k == 3:
+                cap(0, 0)
+                cap(0, 1)
+                quant(0, 0)
+                quant(0, 1)
+        for k in range(FIRST, TILES):
+            h[k] = keep.tile([P, S], F32, name="h%d" % k, tag="h%d" % (k - FIRST))
+            for c in range(CHUNKS):
+                raw_cost(k, c)
+        readout(0, 0)
+        readout(0, 1)
+        for k in range(FIRST, TILES - 1):
+            softplus(k)
+            pick(k, 0, M)
+        last = TILES - 1
+        softplus(last)
+        pick(last, 0, BANK)
+        cap(1, 0)
+        pick(last, BANK, M)
+        quant(1, 0)
+        readout(1, 0)
+        cap(1, 1)
+        finish(0, 0)
+        quant(1, 1)
+        readout(1, 1)
+        for t in range(1, 4):
+            finish(0, t)
+        for t in range(4):
+            finish(1, t)

@@ -33,50 +33,59 @@ def tile_list_eclass_cost_extraction_kernel(
 
         idx = keep.tile([P, S // 16], U16, name="idx")
         nc.sync.dma_start(idx[:], offs)
-        w4raw = keep.tile([P, 2 * H], U8, name="w4raw", tag="slot_b")
-        nc.sync.dma_start(w4raw[:].bitcast(I32), w4_words[0].bitcast(I32))
+        w4raw = [
+            keep.tile([P, H], U8, name="w4raw0", tag="slot_a"),
+            keep.tile([P, H], U8, name="w4raw1", tag="slot_d", align_bytes=64),
+        ]
+        nc.sync.dma_start(w4raw[0][:].bitcast(I32), w4_words[0, :, 0:H].bitcast(I32))
         tabw = keep.tile([P, T], I32, name="tabw")
         nc.sync.dma_start(tabw[:], tab_words[0].rearrange("p t i -> p (t i)").bitcast(I32))
+        nc.sync.dma_start(w4raw[1][:].bitcast(I32), w4_words[0, :, H : 2 * H].bitcast(I32))
 
-        tabs = keep.tile([P, T], U8, name="tabs")
+        tabs = keep.tile([P, T], U8, name="tabs", tag="slot_b")
         nc.vector.memset(tabs[:].bitcast(I32), 0)
-        w4sraw = keep.tile([P, H], U8, name="w4sraw", tag="slot_a")
+        w4sraw = keep.tile([P, H], U8, name="w4sraw", tag="slot_c", align_bytes=64)
         nc.gpsimd.memset(w4sraw[:].bitcast(I32), 0)
         for q in range(4):
             nc.scalar.dma_start(tabs[32 * q : 32 * q + 4, :].bitcast(I32), tab_scales[0, 4 * q : 4 * q + 4, :].bitcast(I32))
         for q in range(4):
-            (nc.gpsimd if q < 2 else nc.scalar).dma_start(w4sraw[32 * q : 32 * q + 4, :].bitcast(I32), w4_scales[0, 4 * q : 4 * q + 4, :].bitcast(I32))
+            (nc.gpsimd if q < 3 else nc.scalar).dma_start(
+                w4sraw[32 * q : 32 * q + 4, :].bitcast(I32), w4_scales[0, 4 * q : 4 * q + 4, :].bitcast(I32)
+            )
         gain_sb = keep.tile([P, 2, 4], F32, name="gain_sb")
         nc.gpsimd.dma_start(gain_sb[:], gain.rearrange("(b p i) -> p b i", b=2, i=4))
         idx2 = keep.tile([P, M // 16], U16, name="idx2")
         nc.sync.dma_start(idx2[:], offs2)
 
-        w4w = keep.tile([P, 2 * H], U8, name="w4w", align_bytes=64)
+        w4w = [keep.tile([P, H], U8, name="w4w%d" % b, align_bytes=64) for b in range(2)]
         w4s = keep.tile([P, H], U8, name="w4s", align_bytes=64)
-        nc.vector.tensor_copy(
-            w4w[:].bitcast(U16).rearrange("p (b t m) -> p b t m", b=2, t=4),
-            w4raw[:].bitcast(U16).rearrange("p (b m t) -> p b t m", b=2, t=4),
-        )
+
+        def order_w4(b):
+            nc.vector.tensor_copy(
+                w4w[b][:].bitcast(U16).rearrange("p (t m) -> p t m", t=4),
+                w4raw[b][:].bitcast(U16).rearrange("p (m t) -> p t m", t=4),
+            )
+
+        order_w4(0)
         nc.vector.tensor_copy(
             w4s[:].rearrange("p (b t m) -> p b t m", b=2, t=4),
             w4sraw[:].rearrange("p (b m t) -> p b t m", b=2, t=4),
         )
-        wgt_sb = keep.tile([P, M], F32, name="wgt_sb", tag="slot_b")
-        nc.sync.dma_start(wgt_sb[:], wgt)
         w2raw = keep.tile([P, 2, 4, N], F32, name="w2raw", tag="slot_a")
         nc.sync.dma_start(w2raw[:], w2.rearrange("(b p j) n -> p b j n", b=2, j=4))
 
-        vw, vs = [], []
+        vw = keep.tile([P, S], U32, name="vw", tag="slot_c", align_bytes=64)
+        vs = []
         h = {}
 
         def raw_cost(k, c):
             acc = psum.tile([P, BANK], F32, name="acc", tag="bank")
             nc.tensor.matmul_mx(
                 out=acc[:],
-                lhsT=w4w[:, 2 * P * k : 2 * P * (k + 1)].bitcast(FP4X4),
+                lhsT=w4w[k // 4][:, 2 * P * (k % 4) : 2 * P * (k % 4 + 1)].bitcast(FP4X4),
                 lhsT_scale=w4s[:, P * k : P * (k + 1)],
-                rhs=vw[c][:].bitcast(FP8X4),
-                rhs_scale=vs[c][:],
+                rhs=vw[:, BANK * c : BANK * (c + 1)].bitcast(FP8X4),
+                rhs_scale=vs[c],
                 start=True,
                 stop=True,
             )
@@ -86,13 +95,21 @@ def tile_list_eclass_cost_extraction_kernel(
             h[k] = keep.tile([P, S], F32, name="h%d" % k, tag="h%d" % k)
         for c in range(CHUNKS):
             cols = idx[:, 32 * c : 32 * (c + 1)]
-            vs.append(keep.tile([P, BANK], U8, name="vs%d" % c, align_bytes=64))
-            vw.append(keep.tile([P, BANK], U32, name="vw%d" % c, align_bytes=64))
-            nc.vector.tensor_copy(vs[c][:], tabs[:].indirect(cols))
-            nc.vector.tensor_copy(vw[c][:], tabw[:].bitcast(U32).indirect(cols))
+            if c == 0:
+                vs_early = keep.tile([P, 2 * BANK], U8, name="vs_early", align_bytes=64)
+                vs.extend([vs_early[:, 0:BANK], vs_early[:, BANK : 2 * BANK]])
+            if c == 2:
+                vs_late = keep.tile([P, 2 * BANK], U8, name="vs_late", tag="slot_d", align_bytes=64)
+                vs.extend([vs_late[:, 0:BANK], vs_late[:, BANK : 2 * BANK]])
+            nc.vector.tensor_copy(vs[c], tabs[:].indirect(cols))
+            nc.vector.tensor_copy(vw[:, BANK * c : BANK * (c + 1)], tabw[:].bitcast(U32).indirect(cols))
+            if c == 0:
+                order_w4(1)
             for k in range(FIRST):
                 raw_cost(k, c)
 
+        wgt_sb = keep.tile([P, M], F32, name="wgt_sb", tag="slot_b")
+        nc.sync.dma_start(wgt_sb[:], wgt)
         w2bf = keep.tile([P, 2, N * 4], BF16, name="w2bf", tag="grouped", align_bytes=64)
         w2w = keep.tile([P, 2 * N], U32, name="w2w", align_bytes=64)
         w2s = keep.tile([P, 2 * N], U8, name="w2s", align_bytes=64)

@@ -20,7 +20,7 @@ P = 128
 BANK = 512
 CHUNKS = S // BANK
 TILES = H // P
-FIRST = 6
+FIRST = 5
 
 
 def tile_list_eclass_cost_extraction_kernel(
@@ -110,7 +110,7 @@ def tile_list_eclass_cost_extraction_kernel(
 
         wgt_sb = keep.tile([P, M], F32, name="wgt_sb", tag="slot_b")
         nc.sync.dma_start(wgt_sb[:], wgt)
-        w2bf = keep.tile([P, 2, N * 4], BF16, name="w2bf", tag="grouped", align_bytes=64)
+        w2bf = keep.tile([P, 2, N * 4], BF16, name="w2bf", align_bytes=64)
         w2w = keep.tile([P, 2 * N], U32, name="w2w", align_bytes=64)
         w2s = keep.tile([P, 2 * N], U8, name="w2s", align_bytes=64)
         for b in range(2):
@@ -130,15 +130,10 @@ def tile_list_eclass_cost_extraction_kernel(
             nc.sync.dma_start(bud[b][:], budget[512 * b : 512 * (b + 1), :].rearrange("(p i) m -> p i m", i=4))
         res = []
         x = [keep.tile([P, 4, M], F32, name="x0"), keep.tile([P, 4, M], F32, name="x1")]
+        zw = [keep.tile([P, M], U32, name="zw%d" % b, align_bytes=64) for b in range(2)]
+        zs = [keep.tile([P, M], U8, name="zs%d" % b, align_bytes=64) for b in range(2)]
         z = {}
-        zw, zs = {}, {}
-        zall = keep.tile([P, 2, BANK * 4], BF16, name="zall", tag="grouped", align_bytes=64)
-        for u in range(2):
-            z[0, u] = zall[:, u, :]
-            z[1, u] = keep.tile([P, BANK * 4], BF16, name="z1%d" % u, align_bytes=64)[:]
-            for b in range(2):
-                zw[b, u] = keep.tile([P, BANK], U32, name="zw%d%d" % (b, u), align_bytes=64)
-                zs[b, u] = keep.tile([P, BANK], U8, name="zs%d%d" % (b, u), align_bytes=64)
+        QUARTER = 256
 
         def softplus(k):
             nc.scalar.activation(h[k][:], h[k][:], ACT.Ln, bias=1.0)
@@ -148,37 +143,42 @@ def tile_list_eclass_cost_extraction_kernel(
                 x[k // 4][:, k % 4, m0:m1], h[k][:].indirect(idx2[:, m0 // 16 : m1 // 16]), wg[k][:, m0:m1], ALU.mult
             )
 
-        def cap(b, u):
+        def cap(b, m0, m1):
+            z[b, m0] = keep.tile([P, 4 * (m1 - m0)], BF16, name="z%d_%d" % (b, m0), align_bytes=64)
             nc.vector.tensor_tensor(
-                z[b, u].rearrange("p (c i t) -> p c t i", i=4, t=4),
-                x[b][:, :, BANK * u : BANK * (u + 1)].rearrange("p t (c i) -> p c t i", i=4),
-                bud[b][:, :, BANK * u : BANK * (u + 1)].rearrange("p t (c i) -> p c t i", i=4),
+                z[b, m0][:].rearrange("p (c i t) -> p c t i", i=4, t=4),
+                x[b][:, :, m0:m1].rearrange("p t (c i) -> p c t i", i=4),
+                bud[b][:, :, m0:m1].rearrange("p t (c i) -> p c t i", i=4),
                 ALU.min,
             )
 
-        def quant(b, u):
-            nc.vector.quantize_mx(out=zw[b, u][:].bitcast(FP8X4), scales=zs[b, u][:], in_=z[b, u])
+        def quant(b, m0, m1):
+            nc.vector.quantize_mx(out=zw[b][:, m0:m1].bitcast(FP8X4), scales=zs[b][:, m0:m1], in_=z[b, m0][:])
 
         y = {}
 
-        def readout(b, u):
+        def readout(b, m0):
             for t in range(4):
-                if b == 0:
-                    y[u, t] = psum.tile([P, BANK], F32, name="y", tag="bank")
+                if b == 0 and t % 2 == 0:
+                    y[m0, t // 2] = psum.tile([P, 2, QUARTER], F32, name="y", tag="bank")
                 cols = slice(N * b + P * t, N * b + P * (t + 1))
                 nc.tensor.matmul_mx(
-                    out=y[u, t][:],
+                    out=y[m0, t // 2][:, t % 2, :],
                     lhsT=w2w[:, cols].bitcast(FP8X4),
                     lhsT_scale=w2s[:, cols],
-                    rhs=zw[b, u][:].bitcast(FP8X4),
-                    rhs_scale=zs[b, u][:],
-                    start=(b == 0),
-                    stop=(b == 1),
+                    rhs=zw[b][:, m0 : m0 + QUARTER].bitcast(FP8X4),
+                    rhs_scale=zs[b][:, m0 : m0 + QUARTER],
+                    start=(b == 0 and t % 2 == 0),
+                    stop=(b == 1 and t % 2 == 1),
                 )
 
-        def finish(u, t):
-            nc.vector.tensor_tensor(res[u][:, t, :], y[u, t][:], res[u][:, t, :], ALU.subtract)
-            nc.sync.dma_start(out[P * t : P * (t + 1), BANK * u : BANK * (u + 1)], res[u][:, t, :])
+        def finish(m0):
+            u, c0 = divmod(m0, BANK)
+            for pair in range(2):
+                part = res[u][:, 2 * pair : 2 * pair + 2, c0 : c0 + QUARTER]
+                nc.vector.tensor_tensor(part, y[m0, pair][:], part, ALU.subtract)
+                rows = out[2 * P * pair : 2 * P * (pair + 1), m0 : m0 + QUARTER]
+                nc.sync.dma_start(rows.rearrange("(t p) m -> p t m", p=P), part)
 
         for k in range(FIRST):
             softplus(k)
@@ -187,31 +187,29 @@ def tile_list_eclass_cost_extraction_kernel(
                 res.append(keep.tile([P, 4, BANK], F32, name="res%d" % k, tag="wg%d" % k))
                 nc.sync.dma_start(res[k][:], best[:, BANK * k : BANK * (k + 1)].rearrange("(t p) m -> p t m", p=P))
             if k == 3:
-                cap(0, 0)
-                cap(0, 1)
-                quant(0, 0)
-                quant(0, 1)
+                cap(0, 0, BANK)
+                cap(0, BANK, M)
+                quant(0, 0, BANK)
+                quant(0, BANK, M)
         for k in range(FIRST, TILES):
             h[k] = keep.tile([P, S], F32, name="h%d" % k, tag="h%d" % (k - FIRST))
             for c in range(CHUNKS):
                 raw_cost(k, c)
-        readout(0, 0)
-        readout(0, 1)
+        for m0 in range(0, M, QUARTER):
+            readout(0, m0)
         for k in range(FIRST, TILES - 1):
             softplus(k)
             pick(k, 0, M)
         last = TILES - 1
         softplus(last)
-        pick(last, 0, BANK)
-        cap(1, 0)
-        pick(last, BANK, M)
-        quant(1, 0)
-        readout(1, 0)
-        cap(1, 1)
-        finish(0, 0)
-        quant(1, 1)
-        readout(1, 1)
-        for t in range(1, 4):
-            finish(0, t)
-        for t in range(4):
-            finish(1, t)
+        for step in range(-1, 6):
+            m0 = QUARTER * step
+            if step + 1 < 4:
+                pick(last, m0 + QUARTER, m0 + 2 * QUARTER)
+            if 0 <= step - 1 < 4:
+                quant(1, m0 - QUARTER, m0)
+                readout(1, m0 - QUARTER)
+            if 0 <= step < 4:
+                cap(1, m0, m0 + QUARTER)
+            if 0 <= step - 2 < 4:
+                finish(m0 - 2 * QUARTER)

@@ -20,7 +20,7 @@ P = 128
 BANK = 512
 CHUNKS = S // BANK
 TILES = H // P
-FIRST = 5
+FIRST = 6
 
 
 def tile_list_eclass_cost_extraction_kernel(
@@ -31,51 +31,63 @@ def tile_list_eclass_cost_extraction_kernel(
         keep = ctx.enter_context(tc.tile_pool(name="keep", bufs=1))
         psum = ctx.enter_context(tc.psum_pool(name="psum", bufs=8))
 
+        head = ctx.enter_context(tc.tile_pool(name="head", bufs=1))
+
+        def placed(shape, dtype, name, offset):
+            return head.tile(shape, dtype, name=name, offset=offset, align_bytes=64)
+
         idx = keep.tile([P, S // 16], U16, name="idx")
         nc.sync.dma_start(idx[:], offs)
-        w4raw = [
-            keep.tile([P, H], U8, name="w4raw0", tag="slot_a"),
-            keep.tile([P, H], U8, name="w4raw1", tag="slot_d", align_bytes=64),
-        ]
-        nc.sync.dma_start(w4raw[0][:].bitcast(I32), w4_words[0, :, 0:H].bitcast(I32))
+        w4raw = keep.tile([P, 2 * H], U8, name="w4raw")
+        nc.scalar.dma_start(w4raw[:].bitcast(I32), w4_words[0].bitcast(I32))
+        idx2 = keep.tile([P, M // 16], U16, name="idx2")
+        nc.sync.dma_start(idx2[:], offs2)
         tabw = keep.tile([P, T], I32, name="tabw")
         nc.sync.dma_start(tabw[:], tab_words[0].rearrange("p t i -> p (t i)").bitcast(I32))
-        nc.sync.dma_start(w4raw[1][:].bitcast(I32), w4_words[0, :, H : 2 * H].bitcast(I32))
 
-        tabs = keep.tile([P, T], U8, name="tabs", tag="slot_b")
-        nc.vector.memset(tabs[:].bitcast(I32), 0)
-        w4sraw = keep.tile([P, H], U8, name="w4sraw", tag="slot_c", align_bytes=64)
+        tabs_a = placed([P, T], U8, "tabs_a", 6144)
+        nc.vector.memset(tabs_a[:].bitcast(I32), 0)
+        nc.scalar.dma_start(tabs_a[0:P:8, :].bitcast(I32), tab_scales[0].bitcast(I32))
+        w4sraw = placed([P, H], U8, "w4sraw", 0)
         nc.gpsimd.memset(w4sraw[:].bitcast(I32), 0)
         for q in range(4):
-            nc.scalar.dma_start(tabs[32 * q : 32 * q + 4, :].bitcast(I32), tab_scales[0, 4 * q : 4 * q + 4, :].bitcast(I32))
-        for q in range(4):
-            (nc.gpsimd if q < 3 else nc.scalar).dma_start(
+            (nc.gpsimd if q < 2 else nc.scalar).dma_start(
                 w4sraw[32 * q : 32 * q + 4, :].bitcast(I32), w4_scales[0, 4 * q : 4 * q + 4, :].bitcast(I32)
             )
         gain_sb = keep.tile([P, 2, 4], F32, name="gain_sb")
         nc.gpsimd.dma_start(gain_sb[:], gain.rearrange("(b p i) -> p b i", b=2, i=4))
-        idx2 = keep.tile([P, M // 16], U16, name="idx2")
-        nc.sync.dma_start(idx2[:], offs2)
+        vs_early = keep.tile([P, 2 * BANK], U8, name="vs_early", align_bytes=64)
+        nc.vector.memset(vs_early[:].bitcast(I32), 0)
 
-        w4w = [keep.tile([P, H], U8, name="w4w%d" % b, align_bytes=64) for b in range(2)]
-        w4s = keep.tile([P, H], U8, name="w4s", align_bytes=64)
+        w4w = [keep.tile([P, H], U8, name="w4w0", align_bytes=64), placed([P, H], U8, "w4w1", 8192)]
+        w4s = placed([P, H], U8, "w4s", 9216)
 
         def order_w4(b):
             nc.vector.tensor_copy(
                 w4w[b][:].bitcast(U16).rearrange("p (t m) -> p t m", t=4),
-                w4raw[b][:].bitcast(U16).rearrange("p (m t) -> p t m", t=4),
+                w4raw[:, H * b : H * (b + 1)].bitcast(U16).rearrange("p (m t) -> p t m", t=4),
             )
 
         order_w4(0)
+        LOW, HIGH = 10240, 10240 + 16384 + 1536
+        spread = placed([P, 2 * BANK], U8, "spread", LOW + 16384 - 256)
+        nc.vector.tensor_copy(spread[:], tabs_a[:].indirect(idx[:, 0:64]))
+        for q in range(4):
+            nc.scalar.dma_start(vs_early[32 * q : 32 * q + 4, :].bitcast(I32), spread[32 * q : 32 * q + 32 : 8, :].bitcast(I32))
+        tabs = placed([P, T], U8, "tabs_b", HIGH)
+        nc.vector.tensor_copy(tabs[:].bitcast(I32), tabs_a[:].bitcast(I32))
+        order_w4(1)
         nc.vector.tensor_copy(
             w4s[:].rearrange("p (b t m) -> p b t m", b=2, t=4),
             w4sraw[:].rearrange("p (b m t) -> p b t m", b=2, t=4),
         )
-        w2raw = keep.tile([P, 2, 4, N], F32, name="w2raw", tag="slot_a")
+        w2raw = placed([P, 2, 4, N], F32, "w2raw", LOW)
         nc.sync.dma_start(w2raw[:], w2.rearrange("(b p j) n -> p b j n", b=2, j=4))
 
-        vw = keep.tile([P, S], U32, name="vw", tag="slot_c", align_bytes=64)
-        vs = []
+        vw = placed([P, S], U32, "vw", 0)
+        vs_late = keep.tile([P, 2 * BANK], U8, name="vs_late", align_bytes=64)
+        nc.gpsimd.memset(vs_late[:].bitcast(I32), 0)
+        vs = [vs_early[:, 0:BANK], vs_early[:, BANK : 2 * BANK], vs_late[:, 0:BANK], vs_late[:, BANK : 2 * BANK]]
         h = {}
 
         def raw_cost(k, c):
@@ -95,20 +107,16 @@ def tile_list_eclass_cost_extraction_kernel(
             h[k] = keep.tile([P, S], F32, name="h%d" % k, tag="h%d" % k)
         for c in range(CHUNKS):
             cols = idx[:, 32 * c : 32 * (c + 1)]
-            if c == 0:
-                vs_early = keep.tile([P, 2 * BANK], U8, name="vs_early", align_bytes=64)
-                vs.extend([vs_early[:, 0:BANK], vs_early[:, BANK : 2 * BANK]])
-            if c == 2:
-                vs_late = keep.tile([P, 2 * BANK], U8, name="vs_late", tag="slot_d", align_bytes=64)
-                vs.extend([vs_late[:, 0:BANK], vs_late[:, BANK : 2 * BANK]])
-            nc.vector.tensor_copy(vs[c], tabs[:].indirect(cols))
             nc.vector.tensor_copy(vw[:, BANK * c : BANK * (c + 1)], tabw[:].bitcast(U32).indirect(cols))
-            if c == 0:
-                order_w4(1)
+            if c >= 2:
+                late = placed([P, BANK], U8, "late%d" % c, LOW + 16384 + BANK * (c - 2))
+                nc.vector.tensor_copy(late[:], tabs[:].indirect(cols))
+                for q in range(4):
+                    nc.sync.dma_start(vs[c][32 * q : 32 * q + 4, :].bitcast(I32), late[32 * q : 32 * q + 32 : 8, :].bitcast(I32))
             for k in range(FIRST):
                 raw_cost(k, c)
 
-        wgt_sb = keep.tile([P, M], F32, name="wgt_sb", tag="slot_b")
+        wgt_sb = placed([P, M], F32, "wgt_sb", HIGH)
         nc.sync.dma_start(wgt_sb[:], wgt)
         w2bf = keep.tile([P, 2, N * 4], BF16, name="w2bf", align_bytes=64)
         w2w = keep.tile([P, 2 * N], U32, name="w2w", align_bytes=64)
@@ -126,7 +134,7 @@ def tile_list_eclass_cost_extraction_kernel(
 
         bud = []
         for b in range(2):
-            bud.append(keep.tile([P, 4, M], F32, name="bud%d" % b, tag=("slot_a", "slot_b")[b]))
+            bud.append(placed([P, 4, M], F32, "bud%d" % b, (LOW, HIGH)[b]))
             nc.sync.dma_start(bud[b][:], budget[512 * b : 512 * (b + 1), :].rearrange("(p i) m -> p i m", i=4))
         res = []
         x = [keep.tile([P, 4, M], F32, name="x0"), keep.tile([P, 4, M], F32, name="x1")]
@@ -150,6 +158,26 @@ def tile_list_eclass_cost_extraction_kernel(
                 x[b][:, :, m0:m1].rearrange("p t (c i) -> p c t i", i=4),
                 bud[b][:, :, m0:m1].rearrange("p t (c i) -> p c t i", i=4),
                 ALU.min,
+            )
+
+        pairs = {}
+
+        def cap_pair(u, m0):
+            if u == 0:
+                pairs[m0] = keep.tile([P, 2, 2 * QUARTER], BF16, name="pairs%d" % m0)
+            cols = slice(m0, m0 + QUARTER)
+            nc.vector.tensor_tensor(
+                pairs[m0][:, u, :].rearrange("p (c i t) -> p c t i", i=4, t=2),
+                x[1][:, 2 * u : 2 * u + 2, cols].rearrange("p t (c i) -> p c t i", i=4),
+                bud[1][:, 2 * u : 2 * u + 2, cols].rearrange("p t (c i) -> p c t i", i=4),
+                ALU.min,
+            )
+
+        def weave(m0):
+            z[1, m0] = keep.tile([P, 4 * QUARTER], BF16, name="z1_%d" % m0, align_bytes=64)
+            nc.scalar.copy(
+                z[1, m0][:].bitcast(U32).rearrange("p (c i u) -> p c u i", i=4, u=2),
+                pairs[m0][:].rearrange("p u c -> p (u c)").bitcast(U32).rearrange("p (u c i) -> p c u i", u=2, i=4),
             )
 
         def quant(b, m0, m1):
@@ -191,6 +219,8 @@ def tile_list_eclass_cost_extraction_kernel(
                 cap(0, BANK, M)
                 quant(0, 0, BANK)
                 quant(0, BANK, M)
+        for m0 in range(0, M, QUARTER):
+            cap_pair(0, m0)
         for k in range(FIRST, TILES):
             h[k] = keep.tile([P, S], F32, name="h%d" % k, tag="h%d" % (k - FIRST))
             for c in range(CHUNKS):
@@ -202,14 +232,14 @@ def tile_list_eclass_cost_extraction_kernel(
             pick(k, 0, M)
         last = TILES - 1
         softplus(last)
-        for step in range(-1, 6):
-            m0 = QUARTER * step
-            if step + 1 < 4:
-                pick(last, m0 + QUARTER, m0 + 2 * QUARTER)
+        for step in range(7):
+            if step < 4:
+                pick(last, QUARTER * step, QUARTER * (step + 1))
             if 0 <= step - 1 < 4:
-                quant(1, m0 - QUARTER, m0)
-                readout(1, m0 - QUARTER)
-            if 0 <= step < 4:
-                cap(1, m0, m0 + QUARTER)
+                cap_pair(1, QUARTER * (step - 1))
+                weave(QUARTER * (step - 1))
             if 0 <= step - 2 < 4:
-                finish(m0 - 2 * QUARTER)
+                quant(1, QUARTER * (step - 2), QUARTER * (step - 1))
+                readout(1, QUARTER * (step - 2))
+            if 0 <= step - 3 < 4:
+                finish(QUARTER * (step - 3))

@@ -42,10 +42,10 @@ def tile_list_eclass_cost_extraction_kernel(
         nc.scalar.dma_start(w4raw[:].bitcast(I32), w4_words[0].bitcast(I32))
         idx2 = keep.tile([P, M // 16], U16, name="idx2")
         nc.sync.dma_start(idx2[:], offs2)
-        tabw = keep.tile([P, T], I32, name="tabw")
+        tabw = keep.tile([P, T], I32, name="tabw", tag="tabw")
         nc.sync.dma_start(tabw[:], tab_words[0].rearrange("p t i -> p (t i)").bitcast(I32))
 
-        tabs_a = placed([P, T], U8, "tabs_a", 6144)
+        tabs_a = placed([P, T], U8, "tabs_a", 2560)
         nc.vector.memset(tabs_a[:].bitcast(I32), 0)
         nc.scalar.dma_start(tabs_a[0:P:8, :].bitcast(I32), tab_scales[0].bitcast(I32))
         w4sraw = placed([P, H], U8, "w4sraw", 0)
@@ -59,8 +59,8 @@ def tile_list_eclass_cost_extraction_kernel(
         vs_early = keep.tile([P, 2 * BANK], U8, name="vs_early", align_bytes=64)
         nc.vector.memset(vs_early[:].bitcast(I32), 0)
 
-        w4w = [keep.tile([P, H], U8, name="w4w0", align_bytes=64), placed([P, H], U8, "w4w1", 8192)]
-        w4s = placed([P, H], U8, "w4s", 9216)
+        w4w = [keep.tile([P, H], U8, name="w4w0", align_bytes=64), placed([P, H], U8, "w4w1", 4608)]
+        w4s = placed([P, H], U8, "w4s", 5632)
 
         def order_w4(b):
             nc.vector.tensor_copy(
@@ -69,12 +69,14 @@ def tile_list_eclass_cost_extraction_kernel(
             )
 
         order_w4(0)
-        LOW, HIGH = 10240, 10240 + 16384 + 1536
-        spread = placed([P, 2 * BANK], U8, "spread", LOW + 16384 - 256)
-        nc.vector.tensor_copy(spread[:], tabs_a[:].indirect(idx[:, 0:64]))
+        LOW = 6656
+        LATE = LOW + 16384
+        HIGH = LATE + 5120
+        spread = placed([P, 2 * BANK + 128], U8, "spread", LATE - 64)
+        nc.vector.tensor_copy(spread[:, 0 : 2 * BANK], tabs_a[:].indirect(idx[:, 0:64]))
         for q in range(4):
-            nc.scalar.dma_start(vs_early[32 * q : 32 * q + 4, :].bitcast(I32), spread[32 * q : 32 * q + 32 : 8, :].bitcast(I32))
-        tabs = placed([P, T], U8, "tabs_b", HIGH)
+            nc.scalar.dma_start(vs_early[32 * q : 32 * q + 4, :].bitcast(I32), spread[32 * q : 32 * q + 32 : 8, 0 : 2 * BANK].bitcast(I32))
+        tabs = placed([P, T], U8, "tabs_b", HIGH + 2048)
         nc.vector.tensor_copy(tabs[:].bitcast(I32), tabs_a[:].bitcast(I32))
         order_w4(1)
         nc.vector.tensor_copy(
@@ -84,7 +86,7 @@ def tile_list_eclass_cost_extraction_kernel(
         w2raw = placed([P, 2, 4, N], F32, "w2raw", LOW)
         nc.sync.dma_start(w2raw[:], w2.rearrange("(b p j) n -> p b j n", b=2, j=4))
 
-        vw = placed([P, S], U32, "vw", 0)
+        vw = [placed([P, 2 * BANK], U32, "vw_early", 512)]
         vs_late = keep.tile([P, 2 * BANK], U8, name="vs_late", align_bytes=64)
         nc.gpsimd.memset(vs_late[:].bitcast(I32), 0)
         vs = [vs_early[:, 0:BANK], vs_early[:, BANK : 2 * BANK], vs_late[:, 0:BANK], vs_late[:, BANK : 2 * BANK]]
@@ -96,7 +98,7 @@ def tile_list_eclass_cost_extraction_kernel(
                 out=acc[:],
                 lhsT=w4w[k // 4][:, 2 * P * (k % 4) : 2 * P * (k % 4 + 1)].bitcast(FP4X4),
                 lhsT_scale=w4s[:, P * k : P * (k + 1)],
-                rhs=vw[:, BANK * c : BANK * (c + 1)].bitcast(FP8X4),
+                rhs=vw[c // 2][:, BANK * (c % 2) : BANK * (c % 2 + 1)].bitcast(FP8X4),
                 rhs_scale=vs[c],
                 start=True,
                 stop=True,
@@ -107,12 +109,14 @@ def tile_list_eclass_cost_extraction_kernel(
             h[k] = keep.tile([P, S], F32, name="h%d" % k, tag="h%d" % k)
         for c in range(CHUNKS):
             cols = idx[:, 32 * c : 32 * (c + 1)]
-            nc.vector.tensor_copy(vw[:, BANK * c : BANK * (c + 1)], tabw[:].bitcast(U32).indirect(cols))
             if c >= 2:
-                late = placed([P, BANK], U8, "late%d" % c, LOW + 16384 + BANK * (c - 2))
+                late = placed([P, BANK], U8, "late%d" % c, LATE + BANK * (c - 2))
                 nc.vector.tensor_copy(late[:], tabs[:].indirect(cols))
                 for q in range(4):
                     nc.sync.dma_start(vs[c][32 * q : 32 * q + 4, :].bitcast(I32), late[32 * q : 32 * q + 32 : 8, :].bitcast(I32))
+            if c == 2:
+                vw.append(placed([P, 2 * BANK], U32, "vw_late", LATE + 2 * BANK))
+            nc.vector.tensor_copy(vw[c // 2][:, BANK * (c % 2) : BANK * (c % 2 + 1)], tabw[:].bitcast(U32).indirect(cols))
             for k in range(FIRST):
                 raw_cost(k, c)
 
@@ -132,10 +136,15 @@ def tile_list_eclass_cost_extraction_kernel(
             nc.vector.tensor_scalar(wg[k][:], wgt_sb[:], gain_sb[:, k // 4, k % 4 : k % 4 + 1], None, ALU.mult)
         nc.vector.quantize_mx(out=w2w[:].bitcast(FP8X4), scales=w2s[:], in_=w2bf[:].rearrange("p b c -> p (b c)"))
 
-        bud = []
-        for b in range(2):
-            bud.append(placed([P, 4, M], F32, "bud%d" % b, (LOW, HIGH)[b]))
+        bud = {}
+        for b in (1, 0):
+            bud[b] = placed([P, 4, M], F32, "bud%d" % b, (LOW, HIGH + 4096)[b])
             nc.sync.dma_start(bud[b][:], budget[512 * b : 512 * (b + 1), :].rearrange("(p i) m -> p i m", i=4))
+        bud_bf = keep.tile([P, 4 * M], BF16, name="bud_bf", tag="tabw")
+        nc.vector.tensor_copy(
+            bud_bf[:].rearrange("p (c i t) -> p c t i", i=4, t=4),
+            bud[1][:].rearrange("p t (c i) -> p c t i", i=4),
+        )
         res = []
         x = [keep.tile([P, 4, M], F32, name="x0"), keep.tile([P, 4, M], F32, name="x1")]
         zw = [keep.tile([P, M], U32, name="zw%d" % b, align_bytes=64) for b in range(2)]
@@ -160,25 +169,15 @@ def tile_list_eclass_cost_extraction_kernel(
                 ALU.min,
             )
 
-        pairs = {}
-
-        def cap_pair(u, m0):
-            if u == 0:
-                pairs[m0] = keep.tile([P, 2, 2 * QUARTER], BF16, name="pairs%d" % m0)
-            cols = slice(m0, m0 + QUARTER)
-            nc.vector.tensor_tensor(
-                pairs[m0][:, u, :].rearrange("p (c i t) -> p c t i", i=4, t=2),
-                x[1][:, 2 * u : 2 * u + 2, cols].rearrange("p t (c i) -> p c t i", i=4),
-                bud[1][:, 2 * u : 2 * u + 2, cols].rearrange("p t (c i) -> p c t i", i=4),
-                ALU.min,
-            )
-
         def weave(m0):
             z[1, m0] = keep.tile([P, 4 * QUARTER], BF16, name="z1_%d" % m0, align_bytes=64)
             nc.scalar.copy(
-                z[1, m0][:].bitcast(U32).rearrange("p (c i u) -> p c u i", i=4, u=2),
-                pairs[m0][:].rearrange("p u c -> p (u c)").bitcast(U32).rearrange("p (u c i) -> p c u i", u=2, i=4),
+                z[1, m0][:].rearrange("p (c i t) -> p c t i", i=4, t=4),
+                x[1][:, :, m0 : m0 + QUARTER].rearrange("p t (c i) -> p c t i", i=4),
             )
+
+        def cap_rounded(m0):
+            nc.vector.tensor_tensor(z[1, m0][:], z[1, m0][:], bud_bf[:, 4 * m0 : 4 * (m0 + QUARTER)], ALU.min)
 
         def quant(b, m0, m1):
             nc.vector.quantize_mx(out=zw[b][:, m0:m1].bitcast(FP8X4), scales=zs[b][:, m0:m1], in_=z[b, m0][:])
@@ -219,8 +218,6 @@ def tile_list_eclass_cost_extraction_kernel(
                 cap(0, BANK, M)
                 quant(0, 0, BANK)
                 quant(0, BANK, M)
-        for m0 in range(0, M, QUARTER):
-            cap_pair(0, m0)
         for k in range(FIRST, TILES):
             h[k] = keep.tile([P, S], F32, name="h%d" % k, tag="h%d" % (k - FIRST))
             for c in range(CHUNKS):
@@ -232,14 +229,14 @@ def tile_list_eclass_cost_extraction_kernel(
             pick(k, 0, M)
         last = TILES - 1
         softplus(last)
-        for step in range(7):
+        for step in range(8):
             if step < 4:
                 pick(last, QUARTER * step, QUARTER * (step + 1))
-            if 0 <= step - 1 < 4:
-                cap_pair(1, QUARTER * (step - 1))
-                weave(QUARTER * (step - 1))
+                weave(QUARTER * step)
             if 0 <= step - 2 < 4:
-                quant(1, QUARTER * (step - 2), QUARTER * (step - 1))
-                readout(1, QUARTER * (step - 2))
+                cap_rounded(QUARTER * (step - 2))
             if 0 <= step - 3 < 4:
-                finish(QUARTER * (step - 3))
+                quant(1, QUARTER * (step - 3), QUARTER * (step - 2))
+                readout(1, QUARTER * (step - 3))
+            if 0 <= step - 4 < 4:
+                finish(QUARTER * (step - 4))

@@ -38,6 +38,8 @@ def tile_list_eclass_cost_extraction_kernel(
 
         idx = keep.tile([P, S // 16], U16, name="idx")
         nc.sync.dma_start(idx[:], offs)
+        rows16 = keep.tile([16, T], U8, name="rows16")
+        nc.scalar.dma_start(rows16[:].bitcast(I32), tab_scales[0].bitcast(I32))
         w4raw = keep.tile([P, 2 * H], U8, name="w4raw")
         nc.scalar.dma_start(w4raw[:].bitcast(I32), w4_words[0].bitcast(I32))
         idx2 = keep.tile([P, M // 16], U16, name="idx2")
@@ -45,13 +47,16 @@ def tile_list_eclass_cost_extraction_kernel(
         tabw = keep.tile([P, T], I32, name="tabw", tag="tabw")
         nc.sync.dma_start(tabw[:], tab_words[0].rearrange("p t i -> p (t i)").bitcast(I32))
 
-        tabs_a = placed([P, T], U8, "tabs_a", 2560)
-        nc.vector.memset(tabs_a[:].bitcast(I32), 0)
-        nc.scalar.dma_start(tabs_a[0:P:8, :].bitcast(I32), tab_scales[0].bitcast(I32))
+        LOW = 4608
+        LATE = LOW + 16384
+        HIGH = LATE + 5120
+        tabs = placed([P, T], U8, "tabs", HIGH + 2048)
+        nc.vector.memset(tabs[:].bitcast(I32), 0)
+        nc.vector.tensor_copy(tabs[0:16, :].bitcast(I32), rows16[:].bitcast(I32))
         w4sraw = placed([P, H], U8, "w4sraw", 0)
         nc.gpsimd.memset(w4sraw[:].bitcast(I32), 0)
         for q in range(4):
-            (nc.gpsimd if q < 2 else nc.scalar).dma_start(
+            (nc.gpsimd if q < 1 else nc.scalar).dma_start(
                 w4sraw[32 * q : 32 * q + 4, :].bitcast(I32), w4_scales[0, 4 * q : 4 * q + 4, :].bitcast(I32)
             )
         gain_sb = keep.tile([P, 2, 4], F32, name="gain_sb")
@@ -59,8 +64,8 @@ def tile_list_eclass_cost_extraction_kernel(
         vs_early = keep.tile([P, 2 * BANK], U8, name="vs_early", align_bytes=64)
         nc.vector.memset(vs_early[:].bitcast(I32), 0)
 
-        w4w = [keep.tile([P, H], U8, name="w4w0", align_bytes=64), placed([P, H], U8, "w4w1", 4608)]
-        w4s = placed([P, H], U8, "w4s", 5632)
+        w4w = [keep.tile([P, H], U8, name="w4w%d" % b, align_bytes=64) for b in range(2)]
+        w4s = keep.tile([P, H], U8, name="w4s", align_bytes=64)
 
         def order_w4(b):
             nc.vector.tensor_copy(
@@ -68,16 +73,11 @@ def tile_list_eclass_cost_extraction_kernel(
                 w4raw[:, H * b : H * (b + 1)].bitcast(U16).rearrange("p (m t) -> p t m", t=4),
             )
 
-        order_w4(0)
-        LOW = 6656
-        LATE = LOW + 16384
-        HIGH = LATE + 5120
         spread = placed([P, 2 * BANK + 128], U8, "spread", LATE - 64)
-        nc.vector.tensor_copy(spread[:, 0 : 2 * BANK], tabs_a[:].indirect(idx[:, 0:64]))
+        nc.vector.tensor_copy(spread[:, 0 : 2 * BANK], tabs[:].indirect(idx[:, 0:64]))
         for q in range(4):
-            nc.scalar.dma_start(vs_early[32 * q : 32 * q + 4, :].bitcast(I32), spread[32 * q : 32 * q + 32 : 8, 0 : 2 * BANK].bitcast(I32))
-        tabs = placed([P, T], U8, "tabs_b", HIGH + 2048)
-        nc.vector.tensor_copy(tabs[:].bitcast(I32), tabs_a[:].bitcast(I32))
+            nc.scalar.dma_start(vs_early[32 * q : 32 * q + 4, :].bitcast(I32), spread[4 * q : 4 * q + 4, 0 : 2 * BANK].bitcast(I32))
+        order_w4(0)
         order_w4(1)
         nc.vector.tensor_copy(
             w4s[:].rearrange("p (b t m) -> p b t m", b=2, t=4),
@@ -113,7 +113,7 @@ def tile_list_eclass_cost_extraction_kernel(
                 late = placed([P, BANK], U8, "late%d" % c, LATE + BANK * (c - 2))
                 nc.vector.tensor_copy(late[:], tabs[:].indirect(cols))
                 for q in range(4):
-                    nc.sync.dma_start(vs[c][32 * q : 32 * q + 4, :].bitcast(I32), late[32 * q : 32 * q + 32 : 8, :].bitcast(I32))
+                    nc.sync.dma_start(vs[c][32 * q : 32 * q + 4, :].bitcast(I32), late[4 * q : 4 * q + 4, :].bitcast(I32))
             if c == 2:
                 vw.append(placed([P, 2 * BANK], U32, "vw_late", LATE + 2 * BANK))
             nc.vector.tensor_copy(vw[c // 2][:, BANK * (c % 2) : BANK * (c % 2 + 1)], tabw[:].bitcast(U32).indirect(cols))

@@ -38,58 +38,65 @@ def tile_list_eclass_cost_extraction_kernel(
 
         idx = keep.tile([P, S // 16], U16, name="idx")
         nc.sync.dma_start(idx[:], offs)
-        rows16 = keep.tile([16, T], U8, name="rows16")
-        nc.scalar.dma_start(rows16[:].bitcast(I32), tab_scales[0].bitcast(I32))
-        w4raw = keep.tile([P, 2 * H], U8, name="w4raw")
-        nc.scalar.dma_start(w4raw[:].bitcast(I32), w4_words[0].bitcast(I32))
-        idx2 = keep.tile([P, M // 16], U16, name="idx2")
-        nc.sync.dma_start(idx2[:], offs2)
+        tab_rows = keep.tile([16, T], U8, name="tab_rows")
+        nc.scalar.dma_start(tab_rows[:].bitcast(I32), tab_scales[0].bitcast(I32))
+        w4_rows = keep.tile([16, H], U8, name="w4_rows")
+        nc.sync.dma_start(w4_rows[:].bitcast(I32), w4_scales[0].bitcast(I32))
+        w4raw = [keep.tile([P, H], U8, name="w4raw%d" % b) for b in range(2)]
+        nc.scalar.dma_start(w4raw[0][:].bitcast(I32), w4_words[0, :, 0:H].bitcast(I32))
         tabw = keep.tile([P, T], I32, name="tabw", tag="tabw")
         nc.sync.dma_start(tabw[:], tab_words[0].rearrange("p t i -> p (t i)").bitcast(I32))
+        nc.sync.dma_start(w4raw[1][:].bitcast(I32), w4_words[0, :, H : 2 * H].bitcast(I32))
+        idx2 = keep.tile([P, M // 16], U16, name="idx2")
+        nc.sync.dma_start(idx2[:], offs2)
+        gain_sb = keep.tile([P, 2, 4], F32, name="gain_sb")
+        nc.sync.dma_start(gain_sb[:], gain.rearrange("(b p i) -> p b i", b=2, i=4))
 
-        LOW = 4608
+        LOW = 0
         LATE = LOW + 16384
         HIGH = LATE + 5120
         tabs = placed([P, T], U8, "tabs", HIGH + 2048)
         nc.vector.memset(tabs[:].bitcast(I32), 0)
-        nc.vector.tensor_copy(tabs[0:16, :].bitcast(I32), rows16[:].bitcast(I32))
-        w4sraw = placed([P, H], U8, "w4sraw", 0)
+        w4sraw = keep.tile([P, H], U8, name="w4sraw")
         nc.gpsimd.memset(w4sraw[:].bitcast(I32), 0)
-        for q in range(4):
-            (nc.gpsimd if q < 1 else nc.scalar).dma_start(
-                w4sraw[32 * q : 32 * q + 4, :].bitcast(I32), w4_scales[0, 4 * q : 4 * q + 4, :].bitcast(I32)
-            )
-        gain_sb = keep.tile([P, 2, 4], F32, name="gain_sb")
-        nc.gpsimd.dma_start(gain_sb[:], gain.rearrange("(b p i) -> p b i", b=2, i=4))
-        vs_early = keep.tile([P, 2 * BANK], U8, name="vs_early", align_bytes=64)
-        nc.vector.memset(vs_early[:].bitcast(I32), 0)
+        planes = [keep.tile([P, 2 * BANK], U8, name="planes%d" % c, align_bytes=64) for c in range(2)]
+        for c in range(2):
+            nc.gpsimd.memset(planes[c][:].bitcast(I32), 0)
+        nc.vector.tensor_copy(tabs[0:16, :].bitcast(I32), tab_rows[:].bitcast(I32))
 
+        def early_scales(c, stage, queue):
+            spread = keep.tile([P, BANK], U8, name="spread%d" % c)
+            nc.vector.tensor_copy(spread[:], tabs[:].indirect(idx[:, 32 * c : 32 * (c + 1)]))
+            if c == 0:
+                nc.vector.tensor_copy(w4sraw[0:16, :].bitcast(I32), w4_rows[:].bitcast(I32))
+            nc.vector.tensor_copy(
+                stage[:, BANK : 2 * BANK].rearrange("p (t m) -> p t m", t=4),
+                w4sraw[:, BANK * c : BANK * (c + 1)].rearrange("p (m t) -> p t m", t=4),
+            )
+            nc.vector.tensor_copy(stage[0:16, 0:BANK].bitcast(I32), spread[0:16, :].bitcast(I32))
+            for q in range(4):
+                queue.dma_start(planes[c][32 * q : 32 * q + 4, :].bitcast(I32), stage[4 * q : 4 * q + 4, 0 : 2 * BANK].bitcast(I32))
+
+        stage0 = keep.tile([P, 2 * BANK], U8, name="stage0")
+        early_scales(0, stage0, nc.scalar)
+        stage1 = placed([P, 2 * BANK + 128], U8, "stage1", LATE - 64)
         w4w = [keep.tile([P, H], U8, name="w4w%d" % b, align_bytes=64) for b in range(2)]
-        w4s = keep.tile([P, H], U8, name="w4s", align_bytes=64)
 
         def order_w4(b):
             nc.vector.tensor_copy(
                 w4w[b][:].bitcast(U16).rearrange("p (t m) -> p t m", t=4),
-                w4raw[:, H * b : H * (b + 1)].bitcast(U16).rearrange("p (m t) -> p t m", t=4),
+                w4raw[b][:].bitcast(U16).rearrange("p (m t) -> p t m", t=4),
             )
 
-        spread = placed([P, 2 * BANK + 128], U8, "spread", LATE - 64)
-        nc.vector.tensor_copy(spread[:, 0 : 2 * BANK], tabs[:].indirect(idx[:, 0:64]))
-        for q in range(4):
-            nc.scalar.dma_start(vs_early[32 * q : 32 * q + 4, :].bitcast(I32), spread[4 * q : 4 * q + 4, 0 : 2 * BANK].bitcast(I32))
         order_w4(0)
-        order_w4(1)
-        nc.vector.tensor_copy(
-            w4s[:].rearrange("p (b t m) -> p b t m", b=2, t=4),
-            w4sraw[:].rearrange("p (b m t) -> p b t m", b=2, t=4),
-        )
+        early_scales(1, stage1, nc.sync)
         w2raw = placed([P, 2, 4, N], F32, "w2raw", LOW)
         nc.sync.dma_start(w2raw[:], w2.rearrange("(b p j) n -> p b j n", b=2, j=4))
 
-        vw = [placed([P, 2 * BANK], U32, "vw_early", 512)]
+        vw = [keep.tile([P, 2 * BANK], U32, name="vw_early", align_bytes=64)]
         vs_late = keep.tile([P, 2 * BANK], U8, name="vs_late", align_bytes=64)
         nc.gpsimd.memset(vs_late[:].bitcast(I32), 0)
-        vs = [vs_early[:, 0:BANK], vs_early[:, BANK : 2 * BANK], vs_late[:, 0:BANK], vs_late[:, BANK : 2 * BANK]]
+        vs = [planes[0][:, 0:BANK], planes[1][:, 0:BANK], vs_late[:, 0:BANK], vs_late[:, BANK : 2 * BANK]]
         h = {}
 
         def raw_cost(k, c):
@@ -97,7 +104,7 @@ def tile_list_eclass_cost_extraction_kernel(
             nc.tensor.matmul_mx(
                 out=acc[:],
                 lhsT=w4w[k // 4][:, 2 * P * (k % 4) : 2 * P * (k % 4 + 1)].bitcast(FP4X4),
-                lhsT_scale=w4s[:, P * k : P * (k + 1)],
+                lhsT_scale=planes[k // 4][:, BANK + P * (k % 4) : BANK + P * (k % 4 + 1)],
                 rhs=vw[c // 2][:, BANK * (c % 2) : BANK * (c % 2 + 1)].bitcast(FP8X4),
                 rhs_scale=vs[c],
                 start=True,
@@ -117,6 +124,8 @@ def tile_list_eclass_cost_extraction_kernel(
             if c == 2:
                 vw.append(placed([P, 2 * BANK], U32, "vw_late", LATE + 2 * BANK))
             nc.vector.tensor_copy(vw[c // 2][:, BANK * (c % 2) : BANK * (c % 2 + 1)], tabw[:].bitcast(U32).indirect(cols))
+            if c == 0:
+                order_w4(1)
             for k in range(FIRST):
                 raw_cost(k, c)
 

@@ -38,7 +38,7 @@ def tile_list_eclass_cost_extraction_kernel(
 
         idx = keep.tile([P, S // 16], U16, name="idx")
         nc.sync.dma_start(idx[:], offs)
-        tab_rows = keep.tile([16, T], U8, name="tab_rows")
+        tab_rows = keep.tile([16, T], U8, name="tab_rows", tag="pairs%d" % BANK)
         nc.scalar.dma_start(tab_rows[:].bitcast(I32), tab_scales[0].bitcast(I32))
         w4_rows = keep.tile([16, H], U8, name="w4_rows")
         nc.sync.dma_start(w4_rows[:].bitcast(I32), w4_scales[0].bitcast(I32))
@@ -149,10 +149,14 @@ def tile_list_eclass_cost_extraction_kernel(
         for b in (1, 0):
             bud[b] = placed([P, 4, M], F32, "bud%d" % b, (LOW, HIGH + 4096)[b])
             nc.sync.dma_start(bud[b][:], budget[512 * b : 512 * (b + 1), :].rearrange("(p i) m -> p i m", i=4))
-        bud_bf = keep.tile([P, 4 * M], BF16, name="bud_bf", tag="tabw")
+        bud_bf = keep.tile([P, 3 * M], BF16, name="bud_bf", tag="tabw")
         nc.vector.tensor_copy(
-            bud_bf[:].rearrange("p (c i t) -> p c t i", i=4, t=4),
-            bud[1][:].rearrange("p t (c i) -> p c t i", i=4),
+            bud_bf[:, 0 : 2 * M].rearrange("p (c i t) -> p c t i", i=4, t=4),
+            bud[1][:, :, 0:BANK].rearrange("p t (c i) -> p c t i", i=4),
+        )
+        nc.vector.tensor_copy(
+            bud_bf[:, 2 * M : 3 * M].rearrange("p (c i t) -> p c t i", i=4, t=2),
+            bud[1][:, 2:4, BANK:M].rearrange("p t (c i) -> p c t i", i=4),
         )
         res = []
         x = [keep.tile([P, 4, M], F32, name="x0"), keep.tile([P, 4, M], F32, name="x1")]
@@ -187,6 +191,35 @@ def tile_list_eclass_cost_extraction_kernel(
 
         def cap_rounded(m0):
             nc.vector.tensor_tensor(z[1, m0][:], z[1, m0][:], bud_bf[:, 4 * m0 : 4 * (m0 + QUARTER)], ALU.min)
+
+        pairs = {}
+
+        def cap_pair(m0):
+            pairs[m0] = keep.tile([P, 2, 2 * QUARTER], BF16, name="pairs%d" % m0, tag="pairs%d" % m0)
+            cols = slice(m0, m0 + QUARTER)
+            nc.vector.tensor_tensor(
+                pairs[m0][:, 0, :].rearrange("p (c i t) -> p c t i", i=4, t=2),
+                x[1][:, 0:2, cols].rearrange("p t (c i) -> p c t i", i=4),
+                bud[1][:, 0:2, cols].rearrange("p t (c i) -> p c t i", i=4),
+                ALU.min,
+            )
+
+        def round_pair(m0):
+            nc.scalar.copy(
+                pairs[m0][:, 1, :].rearrange("p (c i t) -> p c t i", i=4, t=2),
+                x[1][:, 2:4, m0 : m0 + QUARTER].rearrange("p t (c i) -> p c t i", i=4),
+            )
+
+        def cap_rounded_pair(m0):
+            lo = 2 * M + 2 * (m0 - BANK)
+            nc.vector.tensor_tensor(pairs[m0][:, 1, :], pairs[m0][:, 1, :], bud_bf[:, lo : lo + 2 * QUARTER], ALU.min)
+
+        def weave_pairs(m0):
+            z[1, m0] = keep.tile([P, 4 * QUARTER], BF16, name="z1_%d" % m0, align_bytes=64)
+            nc.scalar.copy(
+                z[1, m0][:].bitcast(U32).rearrange("p (c i u) -> p c u i", i=4, u=2),
+                pairs[m0][:].rearrange("p u c -> p (u c)").bitcast(U32).rearrange("p (u c i) -> p c u i", u=2, i=4),
+            )
 
         def quant(b, m0, m1):
             nc.vector.quantize_mx(out=zw[b][:, m0:m1].bitcast(FP8X4), scales=zs[b][:, m0:m1], in_=z[b, m0][:])
@@ -227,6 +260,8 @@ def tile_list_eclass_cost_extraction_kernel(
                 cap(0, BANK, M)
                 quant(0, 0, BANK)
                 quant(0, BANK, M)
+        for m0 in range(BANK, M, QUARTER):
+            cap_pair(m0)
         for k in range(FIRST, TILES):
             h[k] = keep.tile([P, S], F32, name="h%d" % k, tag="h%d" % (k - FIRST))
             for c in range(CHUNKS):
@@ -238,14 +273,26 @@ def tile_list_eclass_cost_extraction_kernel(
             pick(k, 0, M)
         last = TILES - 1
         softplus(last)
-        for step in range(8):
-            if step < 4:
-                pick(last, QUARTER * step, QUARTER * (step + 1))
-                weave(QUARTER * step)
-            if 0 <= step - 2 < 4:
-                cap_rounded(QUARTER * (step - 2))
-            if 0 <= step - 3 < 4:
-                quant(1, QUARTER * (step - 3), QUARTER * (step - 2))
-                readout(1, QUARTER * (step - 3))
-            if 0 <= step - 4 < 4:
-                finish(QUARTER * (step - 4))
+
+        def product(q):
+            quant(1, QUARTER * q, QUARTER * (q + 1))
+            readout(1, QUARTER * q)
+
+        for q in range(4):
+            pick(last, QUARTER * q, QUARTER * (q + 1))
+            if q < 2:
+                weave(QUARTER * q)
+            else:
+                round_pair(QUARTER * q)
+        for q in range(2):
+            cap_rounded(QUARTER * q)
+        for q in range(2):
+            product(q)
+        for q in range(2, 4):
+            cap_rounded_pair(QUARTER * q)
+            weave_pairs(QUARTER * q)
+        finish(0)
+        for q in range(2, 4):
+            product(q)
+        for q in range(1, 4):
+            finish(QUARTER * q)

@@ -32,16 +32,21 @@ def tile_list_eclass_cost_extraction_kernel(
         psum = ctx.enter_context(tc.psum_pool(name="psum", bufs=8))
 
         head = ctx.enter_context(tc.tile_pool(name="head", bufs=1))
+        mid = ctx.enter_context(tc.tile_pool(name="mid", bufs=1))
 
         def placed(shape, dtype, name, offset):
             return head.tile(shape, dtype, name=name, offset=offset, align_bytes=64)
 
+        LOW = 0
+        LATE = LOW + 16384
+        HIGH = LATE + 5120
+        ROWS = P - 16
+        tabs = placed([P, T], U8, "tabs", HIGH + 2048)
+        w4sraw = keep.tile([P, H], U8, name="w4sraw")
         idx = keep.tile([P, S // 16], U16, name="idx")
         nc.sync.dma_start(idx[:], offs)
-        tab_rows = keep.tile([16, T], U8, name="tab_rows", tag="pairs%d" % BANK)
-        nc.scalar.dma_start(tab_rows[:].bitcast(I32), tab_scales[0].bitcast(I32))
-        w4_rows = keep.tile([16, H], U8, name="w4_rows")
-        nc.sync.dma_start(w4_rows[:].bitcast(I32), w4_scales[0].bitcast(I32))
+        nc.scalar.dma_start(tabs[ROWS:P, :].bitcast(I32), tab_scales[0].bitcast(I32))
+        nc.sync.dma_start(w4sraw[ROWS:P, :].bitcast(I32), w4_scales[0].bitcast(I32))
         w4raw = [keep.tile([P, H], U8, name="w4raw%d" % b) for b in range(2)]
         nc.scalar.dma_start(w4raw[0][:].bitcast(I32), w4_words[0, :, 0:H].bitcast(I32))
         tabw = keep.tile([P, T], I32, name="tabw", tag="tabw")
@@ -52,30 +57,22 @@ def tile_list_eclass_cost_extraction_kernel(
         gain_sb = keep.tile([P, 2, 4], F32, name="gain_sb")
         nc.sync.dma_start(gain_sb[:], gain.rearrange("(b p i) -> p b i", b=2, i=4))
 
-        LOW = 0
-        LATE = LOW + 16384
-        HIGH = LATE + 5120
-        tabs = placed([P, T], U8, "tabs", HIGH + 2048)
-        nc.vector.memset(tabs[:].bitcast(I32), 0)
-        w4sraw = keep.tile([P, H], U8, name="w4sraw")
-        nc.gpsimd.memset(w4sraw[:].bitcast(I32), 0)
+        nc.vector.memset(tabs[0:ROWS, :].bitcast(I32), 0)
+        nc.gpsimd.memset(w4sraw[0:ROWS, :].bitcast(I32), 0)
         planes = [keep.tile([P, 2 * BANK], U8, name="planes%d" % c, align_bytes=64) for c in range(2)]
         for c in range(2):
             nc.gpsimd.memset(planes[c][:].bitcast(I32), 0)
-        nc.vector.tensor_copy(tabs[0:16, :].bitcast(I32), tab_rows[:].bitcast(I32))
 
         def early_scales(c, stage, queue):
-            spread = keep.tile([P, BANK], U8, name="spread%d" % c)
+            spread = keep.tile([P, BANK], U8, name="spread%d" % c, tag="spread")
             nc.vector.tensor_copy(spread[:], tabs[:].indirect(idx[:, 32 * c : 32 * (c + 1)]))
-            if c == 0:
-                nc.vector.tensor_copy(w4sraw[0:16, :].bitcast(I32), w4_rows[:].bitcast(I32))
             nc.vector.tensor_copy(
                 stage[:, BANK : 2 * BANK].rearrange("p (t m) -> p t m", t=4),
                 w4sraw[:, BANK * c : BANK * (c + 1)].rearrange("p (m t) -> p t m", t=4),
             )
-            nc.vector.tensor_copy(stage[0:16, 0:BANK].bitcast(I32), spread[0:16, :].bitcast(I32))
+            nc.vector.tensor_copy(stage[96:P, 0:BANK].bitcast(I32), spread[96:P, :].bitcast(I32))
             for q in range(4):
-                queue.dma_start(planes[c][32 * q : 32 * q + 4, :].bitcast(I32), stage[4 * q : 4 * q + 4, 0 : 2 * BANK].bitcast(I32))
+                queue.dma_start(planes[c][32 * q : 32 * q + 4, :].bitcast(I32), stage[ROWS + 4 * q : ROWS + 4 * q + 4, 0 : 2 * BANK].bitcast(I32))
 
         stage0 = keep.tile([P, 2 * BANK], U8, name="stage0")
         early_scales(0, stage0, nc.scalar)
@@ -120,7 +117,7 @@ def tile_list_eclass_cost_extraction_kernel(
                 late = placed([P, BANK], U8, "late%d" % c, LATE + BANK * (c - 2))
                 nc.vector.tensor_copy(late[:], tabs[:].indirect(cols))
                 for q in range(4):
-                    nc.sync.dma_start(vs[c][32 * q : 32 * q + 4, :].bitcast(I32), late[4 * q : 4 * q + 4, :].bitcast(I32))
+                    nc.sync.dma_start(vs[c][32 * q : 32 * q + 4, :].bitcast(I32), late[ROWS + 4 * q : ROWS + 4 * q + 4, :].bitcast(I32))
             if c == 2:
                 vw.append(placed([P, 2 * BANK], U32, "vw_late", LATE + 2 * BANK))
             nc.vector.tensor_copy(vw[c // 2][:, BANK * (c % 2) : BANK * (c % 2 + 1)], tabw[:].bitcast(U32).indirect(cols))
@@ -141,7 +138,7 @@ def tile_list_eclass_cost_extraction_kernel(
             )
         wg = []
         for k in range(TILES):
-            wg.append(keep.tile([P, M], F32, name="wg%d" % k, tag="wg%d" % k))
+            wg.append(mid.tile([P, M], F32, name="wg%d" % k, offset=4 * M * k))
             nc.vector.tensor_scalar(wg[k][:], wgt_sb[:], gain_sb[:, k // 4, k % 4 : k % 4 + 1], None, ALU.mult)
         nc.vector.quantize_mx(out=w2w[:].bitcast(FP8X4), scales=w2s[:], in_=w2bf[:].rearrange("p b c -> p (b c)"))
 
@@ -174,7 +171,7 @@ def tile_list_eclass_cost_extraction_kernel(
             )
 
         def cap(b, m0, m1):
-            z[b, m0] = keep.tile([P, 4 * (m1 - m0)], BF16, name="z%d_%d" % (b, m0), align_bytes=64)
+            z[b, m0] = mid.tile([P, 4 * (m1 - m0)], BF16, name="z%d_%d" % (b, m0), align_bytes=64, offset=4 * M * 3)
             nc.vector.tensor_tensor(
                 z[b, m0][:].rearrange("p (c i t) -> p c t i", i=4, t=4),
                 x[b][:, :, m0:m1].rearrange("p t (c i) -> p c t i", i=4),
@@ -226,48 +223,61 @@ def tile_list_eclass_cost_extraction_kernel(
 
         y = {}
 
-        def readout(b, m0):
-            for t in range(4):
-                if b == 0 and t % 2 == 0:
-                    y[m0, t // 2] = psum.tile([P, 2, QUARTER], F32, name="y", tag="bank")
-                cols = slice(N * b + P * t, N * b + P * (t + 1))
-                nc.tensor.matmul_mx(
-                    out=y[m0, t // 2][:, t % 2, :],
-                    lhsT=w2w[:, cols].bitcast(FP8X4),
-                    lhsT_scale=w2s[:, cols],
-                    rhs=zw[b][:, m0 : m0 + QUARTER].bitcast(FP8X4),
-                    rhs_scale=zs[b][:, m0 : m0 + QUARTER],
-                    start=(b == 0 and t % 2 == 0),
-                    stop=(b == 1 and t % 2 == 1),
-                )
+        def readout_pass(b, m0, m1, t, acc, start, stop):
+            cols = slice(N * b + P * t, N * b + P * (t + 1))
+            nc.tensor.matmul_mx(
+                out=acc,
+                lhsT=w2w[:, cols].bitcast(FP8X4),
+                lhsT_scale=w2s[:, cols],
+                rhs=zw[b][:, m0:m1].bitcast(FP8X4),
+                rhs_scale=zs[b][:, m0:m1],
+                start=start,
+                stop=stop,
+            )
 
-        def finish(m0):
-            u, c0 = divmod(m0, BANK)
+        def readout(b, m0, m1):
+            for t in range(4):
+                if m0 < BANK:
+                    if b == 0 and t % 2 == 0:
+                        y[m0, t // 2] = psum.tile([P, 2, QUARTER], F32, name="y", tag="bank")
+                    readout_pass(b, m0, m1, t, y[m0, t // 2][:, t % 2, :], b == 0 and t % 2 == 0, b == 1 and t % 2 == 1)
+                else:
+                    if b == 0:
+                        y[BANK, t] = psum.tile([P, BANK], F32, name="y", tag="bank")
+                    readout_pass(b, m0, m1, t, y[BANK, t][:, m0 - BANK : m1 - BANK], b == 0, b == 1 and m1 == M)
+
+        def finish_quarter(m0):
             for pair in range(2):
-                part = res[u][:, 2 * pair : 2 * pair + 2, c0 : c0 + QUARTER]
+                part = res[0][:, 2 * pair : 2 * pair + 2, m0 : m0 + QUARTER]
                 nc.vector.tensor_tensor(part, y[m0, pair][:], part, ALU.subtract)
                 rows = out[2 * P * pair : 2 * P * (pair + 1), m0 : m0 + QUARTER]
                 nc.sync.dma_start(rows.rearrange("(t p) m -> p t m", p=P), part)
 
+        def finish_half(t, parts):
+            for j in range(parts):
+                lo, hi = BANK * j // parts, BANK * (j + 1) // parts
+                part = res[1][:, t, lo:hi]
+                nc.vector.tensor_tensor(part, y[BANK, t][:, lo:hi], part, ALU.subtract)
+                nc.sync.dma_start(out[P * t : P * (t + 1), BANK + lo : BANK + hi], part)
+
         for k in range(FIRST):
             softplus(k)
             pick(k, 0, M)
-            if k < 2:
-                res.append(keep.tile([P, 4, BANK], F32, name="res%d" % k, tag="wg%d" % k))
-                nc.sync.dma_start(res[k][:], best[:, BANK * k : BANK * (k + 1)].rearrange("(t p) m -> p t m", p=P))
-            if k == 3:
-                cap(0, 0, BANK)
-                cap(0, BANK, M)
-                quant(0, 0, BANK)
-                quant(0, BANK, M)
+            if k in (2, 3):
+                u = k - 2
+                res.append(keep.tile([P, 4, BANK], F32, name="res%d" % u, tag="h%d" % k))
+                nc.sync.dma_start(res[u][:], best[:, BANK * u : BANK * (u + 1)].rearrange("(t p) m -> p t m", p=P))
+            if k == 4:
+                cap(0, 0, M)
+        quant(0, 0, M)
         for m0 in range(BANK, M, QUARTER):
             cap_pair(m0)
         for k in range(FIRST, TILES):
             h[k] = keep.tile([P, S], F32, name="h%d" % k, tag="h%d" % (k - FIRST))
             for c in range(CHUNKS):
                 raw_cost(k, c)
-        for m0 in range(0, M, QUARTER):
-            readout(0, m0)
+        for m0, m1 in ((0, QUARTER), (QUARTER, BANK), (BANK, M)):
+            readout(0, m0, m1)
         for k in range(FIRST, TILES - 1):
             softplus(k)
             pick(k, 0, M)
@@ -276,7 +286,7 @@ def tile_list_eclass_cost_extraction_kernel(
 
         def product(q):
             quant(1, QUARTER * q, QUARTER * (q + 1))
-            readout(1, QUARTER * q)
+            readout(1, QUARTER * q, QUARTER * (q + 1))
 
         for q in range(4):
             pick(last, QUARTER * q, QUARTER * (q + 1))
@@ -291,8 +301,9 @@ def tile_list_eclass_cost_extraction_kernel(
         for q in range(2, 4):
             cap_rounded_pair(QUARTER * q)
             weave_pairs(QUARTER * q)
-        finish(0)
+        finish_quarter(0)
         for q in range(2, 4):
             product(q)
-        for q in range(1, 4):
-            finish(QUARTER * q)
+        finish_quarter(QUARTER)
+        for t in range(4):
+            finish_half(t, 2 if t >= 2 else 1)

@@ -37,9 +37,9 @@ def tile_list_eclass_cost_extraction_kernel(
         def placed(shape, dtype, name, offset):
             return head.tile(shape, dtype, name=name, offset=offset, align_bytes=64)
 
-        LOW = 0
-        LATE = LOW + 16384
-        HIGH = LATE + 5120
+        LATE = 4096
+        LOW = 5440
+        HIGH = LOW + 16384
         ROWS = P - 16
         tabs = placed([P, T], U8, "tabs", HIGH + 2048)
         w4sraw = keep.tile([P, H], U8, name="w4sraw")
@@ -48,10 +48,10 @@ def tile_list_eclass_cost_extraction_kernel(
         nc.scalar.dma_start(tabs[ROWS:P, :].bitcast(I32), tab_scales[0].bitcast(I32))
         nc.sync.dma_start(w4sraw[ROWS:P, :].bitcast(I32), w4_scales[0].bitcast(I32))
         w4raw = [keep.tile([P, H], U8, name="w4raw%d" % b) for b in range(2)]
-        nc.scalar.dma_start(w4raw[0][:].bitcast(I32), w4_words[0, :, 0:H].bitcast(I32))
         tabw = keep.tile([P, T], I32, name="tabw", tag="tabw")
         nc.sync.dma_start(tabw[:], tab_words[0].rearrange("p t i -> p (t i)").bitcast(I32))
-        nc.sync.dma_start(w4raw[1][:].bitcast(I32), w4_words[0, :, H : 2 * H].bitcast(I32))
+        for b in range(2):
+            nc.sync.dma_start(w4raw[b][:].bitcast(I32), w4_words[0, :, H * b : H * (b + 1)].bitcast(I32))
         idx2 = keep.tile([P, M // 16], U16, name="idx2")
         nc.sync.dma_start(idx2[:], offs2)
         gain_sb = keep.tile([P, 2, 4], F32, name="gain_sb")
@@ -64,7 +64,7 @@ def tile_list_eclass_cost_extraction_kernel(
             nc.gpsimd.memset(planes[c][:].bitcast(I32), 0)
 
         def early_scales(c, stage, queue):
-            spread = keep.tile([P, BANK], U8, name="spread%d" % c, tag="spread")
+            spread = placed([P, BANK], U8, "spread%d" % c, HIGH - BANK)
             nc.vector.tensor_copy(spread[:], tabs[:].indirect(idx[:, 32 * c : 32 * (c + 1)]))
             nc.vector.tensor_copy(
                 stage[:, BANK : 2 * BANK].rearrange("p (t m) -> p t m", t=4),
@@ -76,19 +76,23 @@ def tile_list_eclass_cost_extraction_kernel(
 
         stage0 = keep.tile([P, 2 * BANK], U8, name="stage0")
         early_scales(0, stage0, nc.scalar)
-        stage1 = placed([P, 2 * BANK + 128], U8, "stage1", LATE - 64)
+        stage1 = placed([P, 2 * BANK], U8, "stage1", LATE - 64)
         w4w = [keep.tile([P, H], U8, name="w4w%d" % b, align_bytes=64) for b in range(2)]
 
-        def order_w4(b):
-            nc.vector.tensor_copy(
-                w4w[b][:].bitcast(U16).rearrange("p (t m) -> p t m", t=4),
-                w4raw[b][:].bitcast(U16).rearrange("p (m t) -> p t m", t=4),
+        for k in range(TILES):
+            b, t = divmod(k, 4)
+            nc.gpsimd.tensor_copy(
+                w4w[b][:, 2 * P * t : 2 * P * (t + 1)].rearrange("p (m e) -> p m e", e=2),
+                w4raw[b][:].rearrange("p (m t e) -> p t m e", t=4, e=2)[:, t, :, :],
             )
-
-        order_w4(0)
         early_scales(1, stage1, nc.sync)
-        w2raw = placed([P, 2, 4, N], F32, "w2raw", LOW)
-        nc.sync.dma_start(w2raw[:], w2.rearrange("(b p j) n -> p b j n", b=2, j=4))
+        w2raw = {}
+
+        def load_w2(b):
+            w2raw[b] = placed([P, 4, N], F32, "w2raw%d" % b, LOW + 8192 * (1 - b))
+            nc.sync.dma_start(w2raw[b][:], w2[512 * b : 512 * (b + 1), :].rearrange("(p j) n -> p j n", j=4))
+
+        load_w2(0)
 
         vw = [keep.tile([P, 2 * BANK], U32, name="vw_early", align_bytes=64)]
         vs_late = keep.tile([P, 2 * BANK], U8, name="vs_late", align_bytes=64)
@@ -114,15 +118,14 @@ def tile_list_eclass_cost_extraction_kernel(
         for c in range(CHUNKS):
             cols = idx[:, 32 * c : 32 * (c + 1)]
             if c >= 2:
-                late = placed([P, BANK], U8, "late%d" % c, LATE + BANK * (c - 2))
+                late = placed([P, BANK], U8, "late%d" % c, LOW - 448 if c == 2 else LATE)
                 nc.vector.tensor_copy(late[:], tabs[:].indirect(cols))
                 for q in range(4):
                     nc.sync.dma_start(vs[c][32 * q : 32 * q + 4, :].bitcast(I32), late[ROWS + 4 * q : ROWS + 4 * q + 4, :].bitcast(I32))
             if c == 2:
-                vw.append(placed([P, 2 * BANK], U32, "vw_late", LATE + 2 * BANK))
+                load_w2(1)
+                vw.append(placed([P, 2 * BANK], U32, "vw_late", 0))
             nc.vector.tensor_copy(vw[c // 2][:, BANK * (c % 2) : BANK * (c % 2 + 1)], tabw[:].bitcast(U32).indirect(cols))
-            if c == 0:
-                order_w4(1)
             for k in range(FIRST):
                 raw_cost(k, c)
 
@@ -134,7 +137,7 @@ def tile_list_eclass_cost_extraction_kernel(
         for b in range(2):
             nc.vector.tensor_copy(
                 w2bf[:, b, :].rearrange("p (c i t) -> p c t i", i=4, t=4),
-                w2raw[:, b, :, :].rearrange("p t (c i) -> p c t i", i=4),
+                w2raw[b][:].rearrange("p t (c i) -> p c t i", i=4),
             )
         wg = []
         for k in range(TILES):

@@ -47,7 +47,7 @@ def tile_list_eclass_cost_extraction_kernel(
         nc.sync.dma_start(idx[:], offs)
         nc.scalar.dma_start(tabs[ROWS:P, :].bitcast(I32), tab_scales[0].bitcast(I32))
         nc.sync.dma_start(w4sraw[ROWS:P, :].bitcast(I32), w4_scales[0].bitcast(I32))
-        w4raw = [keep.tile([P, H], U8, name="w4raw%d" % b) for b in range(2)]
+        w4raw = [placed([P, H], U8, "w4raw0", HIGH - H), keep.tile([P, H], U8, name="w4raw1")]
         tabw = keep.tile([P, T], I32, name="tabw", tag="tabw")
         nc.sync.dma_start(tabw[:], tab_words[0].rearrange("p t i -> p (t i)").bitcast(I32))
         for b in range(2):
@@ -64,7 +64,7 @@ def tile_list_eclass_cost_extraction_kernel(
             nc.gpsimd.memset(planes[c][:].bitcast(I32), 0)
 
         def early_scales(c, stage, queue):
-            spread = placed([P, BANK], U8, "spread%d" % c, HIGH - BANK)
+            spread = keep.tile([P, BANK], U8, name="spread%d" % c, tag="spread")
             nc.vector.tensor_copy(spread[:], tabs[:].indirect(idx[:, 32 * c : 32 * (c + 1)]))
             nc.vector.tensor_copy(
                 stage[:, BANK : 2 * BANK].rearrange("p (t m) -> p t m", t=4),

@@ -1,6 +1,7 @@
 from contextlib import ExitStack
 
 import concourse.mybir as mybir
+from concourse.masks import make_identity
 
 K, T, S, M, H, N = 512, 4096, 2048, 1024, 1024, 512
 FLOPS = 2 * K * H * S + 2 * H * N * M
@@ -18,9 +19,14 @@ ACT = mybir.ActivationFunctionType
 
 P = 128
 BANK = 512
+QUARTER = 256
 CHUNKS = S // BANK
 TILES = H // P
 FIRST = 6
+ROWS = P - 16
+TURNED = (0,)
+TURN0 = 0
+TURN_COLS = QUARTER
 
 
 def tile_list_eclass_cost_extraction_kernel(
@@ -30,7 +36,6 @@ def tile_list_eclass_cost_extraction_kernel(
     with ExitStack() as ctx:
         keep = ctx.enter_context(tc.tile_pool(name="keep", bufs=1))
         psum = ctx.enter_context(tc.psum_pool(name="psum", bufs=8))
-
         head = ctx.enter_context(tc.tile_pool(name="head", bufs=1))
         mid = ctx.enter_context(tc.tile_pool(name="mid", bufs=1))
 
@@ -40,14 +45,14 @@ def tile_list_eclass_cost_extraction_kernel(
         LATE = 4096
         LOW = 5440
         HIGH = LOW + 16384
-        ROWS = P - 16
-        tabs = placed([P, T], U8, "tabs", HIGH + 2048)
+
+        tabs = placed([P, T], U8, "tabs", HIGH + 4096 + 8128)
         w4sraw = keep.tile([P, H], U8, name="w4sraw")
         idx = keep.tile([P, S // 16], U16, name="idx")
         nc.sync.dma_start(idx[:], offs)
         nc.scalar.dma_start(tabs[ROWS:P, :].bitcast(I32), tab_scales[0].bitcast(I32))
         nc.sync.dma_start(w4sraw[ROWS:P, :].bitcast(I32), w4_scales[0].bitcast(I32))
-        w4raw = [placed([P, H], U8, "w4raw0", HIGH - H), keep.tile([P, H], U8, name="w4raw1")]
+        w4raw = [placed([P, H], U8, "w4raw0", HIGH - H // 2), keep.tile([P, H], U8, name="w4raw1", tag="w4raw1")]
         tabw = keep.tile([P, T], I32, name="tabw", tag="tabw")
         nc.sync.dma_start(tabw[:], tab_words[0].rearrange("p t i -> p (t i)").bitcast(I32))
         for b in range(2):
@@ -63,6 +68,10 @@ def tile_list_eclass_cost_extraction_kernel(
         for c in range(2):
             nc.gpsimd.memset(planes[c][:].bitcast(I32), 0)
 
+        def carry(queue, plane, rows):
+            for q in range(4):
+                queue.dma_start(plane[32 * q : 32 * q + 4, :].bitcast(I32), rows[ROWS + 4 * q : ROWS + 4 * q + 4, :].bitcast(I32))
+
         def early_scales(c, stage, queue):
             spread = keep.tile([P, BANK], U8, name="spread%d" % c, tag="spread")
             nc.vector.tensor_copy(spread[:], tabs[:].indirect(idx[:, 32 * c : 32 * (c + 1)]))
@@ -71,14 +80,12 @@ def tile_list_eclass_cost_extraction_kernel(
                 w4sraw[:, BANK * c : BANK * (c + 1)].rearrange("p (m t) -> p t m", t=4),
             )
             nc.vector.tensor_copy(stage[96:P, 0:BANK].bitcast(I32), spread[96:P, :].bitcast(I32))
-            for q in range(4):
-                queue.dma_start(planes[c][32 * q : 32 * q + 4, :].bitcast(I32), stage[ROWS + 4 * q : ROWS + 4 * q + 4, 0 : 2 * BANK].bitcast(I32))
+            carry(queue, planes[c][:], stage[:])
 
         stage0 = keep.tile([P, 2 * BANK], U8, name="stage0")
         early_scales(0, stage0, nc.scalar)
         stage1 = placed([P, 2 * BANK], U8, "stage1", LATE - 64)
         w4w = [keep.tile([P, H], U8, name="w4w%d" % b, align_bytes=64) for b in range(2)]
-
         for k in range(TILES):
             b, t = divmod(k, 4)
             nc.gpsimd.tensor_copy(
@@ -92,11 +99,18 @@ def tile_list_eclass_cost_extraction_kernel(
             w2raw[b] = placed([P, 4, N], F32, "w2raw%d" % b, LOW + 8192 * (1 - b))
             nc.sync.dma_start(w2raw[b][:], w2[512 * b : 512 * (b + 1), :].rearrange("(p j) n -> p j n", j=4))
 
+        wgt_sb = placed([P, M], F32, "wgt_sb", HIGH)
+        nc.sync.dma_start(wgt_sb[:], wgt)
         load_w2(0)
-
+        best_early = keep.tile([P, 2, TURN_COLS], F32, name="best_early", tag="w4raw1")
+        nc.sync.dma_start(best_early[:], best[2 * P : 4 * P, TURN0 : TURN0 + TURN_COLS].rearrange("(t p) m -> p t m", p=P))
         vw = [keep.tile([P, 2 * BANK], U32, name="vw_early", align_bytes=64)]
         vs_late = keep.tile([P, 2 * BANK], U8, name="vs_late", align_bytes=64)
         nc.gpsimd.memset(vs_late[:].bitcast(I32), 0)
+        ident = keep.tile([P, P], F32, name="ident")
+        make_identity(nc, ident[:])
+        minus_one = mid.tile([P, 1], F32, name="minus_one", offset=4 * M * TILES)
+        nc.gpsimd.memset(minus_one[:], -1.0)
         vs = [planes[0][:, 0:BANK], planes[1][:, 0:BANK], vs_late[:, 0:BANK], vs_late[:, BANK : 2 * BANK]]
         h = {}
 
@@ -120,8 +134,7 @@ def tile_list_eclass_cost_extraction_kernel(
             if c >= 2:
                 late = placed([P, BANK], U8, "late%d" % c, LOW - 448 if c == 2 else LATE)
                 nc.vector.tensor_copy(late[:], tabs[:].indirect(cols))
-                for q in range(4):
-                    nc.sync.dma_start(vs[c][32 * q : 32 * q + 4, :].bitcast(I32), late[ROWS + 4 * q : ROWS + 4 * q + 4, :].bitcast(I32))
+                carry(nc.sync, vs[c], late[:])
             if c == 2:
                 load_w2(1)
                 vw.append(placed([P, 2 * BANK], U32, "vw_late", 0))
@@ -129,41 +142,53 @@ def tile_list_eclass_cost_extraction_kernel(
             for k in range(FIRST):
                 raw_cost(k, c)
 
-        wgt_sb = placed([P, M], F32, "wgt_sb", HIGH)
-        nc.sync.dma_start(wgt_sb[:], wgt)
-        w2bf = keep.tile([P, 2, N * 4], BF16, name="w2bf", align_bytes=64)
+        w2bf = keep.tile([P, 2, N * 4], BF16, name="w2bf", tag="w2bf", align_bytes=64)
         w2w = keep.tile([P, 2 * N], U32, name="w2w", align_bytes=64)
         w2s = keep.tile([P, 2 * N], U8, name="w2s", align_bytes=64)
+        wg = []
+        for k in range(TILES):
+            wg.append(mid.tile([P, M], F32, name="wg%d" % k, offset=4 * M * k))
+            nc.vector.tensor_scalar(wg[k][:], wgt_sb[:], gain_sb[:, k // 4, k % 4 : k % 4 + 1], None, ALU.mult)
         for b in range(2):
             nc.vector.tensor_copy(
                 w2bf[:, b, :].rearrange("p (c i t) -> p c t i", i=4, t=4),
                 w2raw[b][:].rearrange("p t (c i) -> p c t i", i=4),
             )
-        wg = []
-        for k in range(TILES):
-            wg.append(mid.tile([P, M], F32, name="wg%d" % k, offset=4 * M * k))
-            nc.vector.tensor_scalar(wg[k][:], wgt_sb[:], gain_sb[:, k // 4, k % 4 : k % 4 + 1], None, ALU.mult)
         nc.vector.quantize_mx(out=w2w[:].bitcast(FP8X4), scales=w2s[:], in_=w2bf[:].rearrange("p b c -> p (b c)"))
 
+        rows1 = budget[512:1024, :].rearrange("(p i) m -> p i m", i=4)
+        bud_whole = placed([P, 4, BANK], F32, "bud_whole", HIGH + 4096)
+        nc.sync.dma_start(bud_whole[:], rows1[:, :, 0:BANK])
+        bud_late = placed([P, 2, BANK], F32, "bud_late", HIGH + 4096 + 8128 + T - 64)
+        nc.sync.dma_start(bud_late[:], rows1[:, 2:4, BANK:M])
+        bud_early = keep.tile([P, 2, BANK], F32, name="bud_early", tag="w2bf", align_bytes=64)
+        nc.sync.dma_start(bud_early[:], rows1[:, 0:2, BANK:M])
         bud = {}
-        for b in (1, 0):
-            bud[b] = placed([P, 4, M], F32, "bud%d" % b, (LOW, HIGH + 4096)[b])
-            nc.sync.dma_start(bud[b][:], budget[512 * b : 512 * (b + 1), :].rearrange("(p i) m -> p i m", i=4))
         bud_bf = keep.tile([P, 3 * M], BF16, name="bud_bf", tag="tabw")
         nc.vector.tensor_copy(
             bud_bf[:, 0 : 2 * M].rearrange("p (c i t) -> p c t i", i=4, t=4),
-            bud[1][:, :, 0:BANK].rearrange("p t (c i) -> p c t i", i=4),
+            bud_whole[:].rearrange("p t (c i) -> p c t i", i=4),
         )
         nc.vector.tensor_copy(
             bud_bf[:, 2 * M : 3 * M].rearrange("p (c i t) -> p c t i", i=4, t=2),
-            bud[1][:, 2:4, BANK:M].rearrange("p t (c i) -> p c t i", i=4),
+            bud_late[:].rearrange("p t (c i) -> p c t i", i=4),
         )
-        res = []
-        x = [keep.tile([P, 4, M], F32, name="x0"), keep.tile([P, 4, M], F32, name="x1")]
+        best_t = {}
+        for m0 in TURNED:
+            turn = psum.tile([P, 2, QUARTER], F32, name="turn", tag="bank")
+            for mb in range(2):
+                for nb in range(2):
+                    lo = m0 - TURN0 + P * mb
+                    nc.tensor.transpose(turn[:, mb, P * nb : P * (nb + 1)], best_early[:, nb, lo : lo + P], ident[:])
+            best_t[m0] = keep.tile([P, 2, QUARTER], F32, name="best_t%d" % m0)
+            nc.vector.tensor_copy(best_t[m0][:], turn[:])
+        bud[0] = placed([P, 4, M], F32, "bud0", LOW)
+        nc.sync.dma_start(bud[0][:], budget[0:512, :].rearrange("(p i) m -> p i m", i=4))
+
+        x = [placed([P, 4, M], F32, "x0", HIGH + 4096), keep.tile([P, 4, M], F32, name="x1")]
         zw = [keep.tile([P, M], U32, name="zw%d" % b, align_bytes=64) for b in range(2)]
         zs = [keep.tile([P, M], U8, name="zs%d" % b, align_bytes=64) for b in range(2)]
         z = {}
-        QUARTER = 256
 
         def softplus(k):
             nc.scalar.activation(h[k][:], h[k][:], ACT.Ln, bias=1.0)
@@ -173,12 +198,12 @@ def tile_list_eclass_cost_extraction_kernel(
                 x[k // 4][:, k % 4, m0:m1], h[k][:].indirect(idx2[:, m0 // 16 : m1 // 16]), wg[k][:, m0:m1], ALU.mult
             )
 
-        def cap(b, m0, m1):
-            z[b, m0] = mid.tile([P, 4 * (m1 - m0)], BF16, name="z%d_%d" % (b, m0), align_bytes=64, offset=4 * M * 3)
+        def cap_first_pass():
+            z[0, 0] = mid.tile([P, 4 * M], BF16, name="z0", align_bytes=64, offset=4 * M * 3)
             nc.vector.tensor_tensor(
-                z[b, m0][:].rearrange("p (c i t) -> p c t i", i=4, t=4),
-                x[b][:, :, m0:m1].rearrange("p t (c i) -> p c t i", i=4),
-                bud[b][:, :, m0:m1].rearrange("p t (c i) -> p c t i", i=4),
+                z[0, 0][:].rearrange("p (c i t) -> p c t i", i=4, t=4),
+                x[0][:].rearrange("p t (c i) -> p c t i", i=4),
+                bud[0][:].rearrange("p t (c i) -> p c t i", i=4),
                 ALU.min,
             )
 
@@ -195,12 +220,12 @@ def tile_list_eclass_cost_extraction_kernel(
         pairs = {}
 
         def cap_pair(m0):
-            pairs[m0] = keep.tile([P, 2, 2 * QUARTER], BF16, name="pairs%d" % m0, tag="pairs%d" % m0)
+            pairs[m0] = mid.tile([P, 2, 2 * QUARTER], BF16, name="pairs%d" % m0, offset=6144 if m0 == BANK else 2048)
             cols = slice(m0, m0 + QUARTER)
             nc.vector.tensor_tensor(
                 pairs[m0][:, 0, :].rearrange("p (c i t) -> p c t i", i=4, t=2),
                 x[1][:, 0:2, cols].rearrange("p t (c i) -> p c t i", i=4),
-                bud[1][:, 0:2, cols].rearrange("p t (c i) -> p c t i", i=4),
+                bud_early[:, :, m0 - BANK : m0 - BANK + QUARTER].rearrange("p t (c i) -> p c t i", i=4),
                 ALU.min,
             )
 
@@ -215,7 +240,7 @@ def tile_list_eclass_cost_extraction_kernel(
             nc.vector.tensor_tensor(pairs[m0][:, 1, :], pairs[m0][:, 1, :], bud_bf[:, lo : lo + 2 * QUARTER], ALU.min)
 
         def weave_pairs(m0):
-            z[1, m0] = keep.tile([P, 4 * QUARTER], BF16, name="z1_%d" % m0, align_bytes=64)
+            z[1, m0] = mid.tile([P, 4 * QUARTER], BF16, name="z1_%d" % m0, align_bytes=64, offset=4 * M * TILES + 8 * (M - QUARTER - m0))
             nc.scalar.copy(
                 z[1, m0][:].bitcast(U32).rearrange("p (c i u) -> p c u i", i=4, u=2),
                 pairs[m0][:].rearrange("p u c -> p (u c)").bitcast(U32).rearrange("p (u c i) -> p c u i", u=2, i=4),
@@ -226,52 +251,84 @@ def tile_list_eclass_cost_extraction_kernel(
 
         y = {}
 
-        def readout_pass(b, m0, m1, t, acc, start, stop):
-            cols = slice(N * b + P * t, N * b + P * (t + 1))
-            nc.tensor.matmul_mx(
-                out=acc,
-                lhsT=w2w[:, cols].bitcast(FP8X4),
-                lhsT_scale=w2s[:, cols],
-                rhs=zw[b][:, m0:m1].bitcast(FP8X4),
-                rhs_scale=zs[b][:, m0:m1],
-                start=start,
-                stop=stop,
-            )
+        def readout(b, m0, which=(0, 1)):
+            for pair in which:
+                if b == 0:
+                    y[m0, pair] = psum.tile([P, 2, QUARTER], F32, name="y", tag="bank")
+                for j in range(2):
+                    if pair == 1 and m0 in TURNED:
+                        still = slice(m0 + P * j, m0 + P * (j + 1))
+                        moving = slice(N * b + QUARTER, N * (b + 1))
+                        lhs, lhs_s, rhs, rhs_s = zw[b][:, still], zs[b][:, still], w2w[:, moving], w2s[:, moving]
+                    else:
+                        still = slice(N * b + P * (2 * pair + j), N * b + P * (2 * pair + j + 1))
+                        moving = slice(m0, m0 + QUARTER)
+                        lhs, lhs_s, rhs, rhs_s = w2w[:, still], w2s[:, still], zw[b][:, moving], zs[b][:, moving]
+                    nc.tensor.matmul_mx(
+                        out=y[m0, pair][:, j, :],
+                        lhsT=lhs.bitcast(FP8X4),
+                        lhsT_scale=lhs_s,
+                        rhs=rhs.bitcast(FP8X4),
+                        rhs_scale=rhs_s,
+                        start=(b == 0 and j == 0),
+                        stop=(b == 1 and j == 1),
+                    )
 
-        def readout(b, m0, m1):
-            for t in range(4):
-                if m0 < BANK:
-                    if b == 0 and t % 2 == 0:
-                        y[m0, t // 2] = psum.tile([P, 2, QUARTER], F32, name="y", tag="bank")
-                    readout_pass(b, m0, m1, t, y[m0, t // 2][:, t % 2, :], b == 0 and t % 2 == 0, b == 1 and t % 2 == 1)
-                else:
-                    if b == 0:
-                        y[BANK, t] = psum.tile([P, BANK], F32, name="y", tag="bank")
-                    readout_pass(b, m0, m1, t, y[BANK, t][:, m0 - BANK : m1 - BANK], b == 0, b == 1 and m1 == M)
+        res = {}
 
-        def finish_quarter(m0):
-            for pair in range(2):
-                part = res[0][:, 2 * pair : 2 * pair + 2, m0 : m0 + QUARTER]
-                nc.vector.tensor_tensor(part, y[m0, pair][:], part, ALU.subtract)
-                rows = out[2 * P * pair : 2 * P * (pair + 1), m0 : m0 + QUARTER]
-                nc.sync.dma_start(rows.rearrange("(t p) m -> p t m", p=P), part)
+        def load_best(m0, pair, tile):
+            res[m0, pair] = tile
+            rows = best[2 * P * pair : 2 * P * (pair + 1), m0 : m0 + QUARTER]
+            nc.sync.dma_start(tile, rows.rearrange("(t p) m -> p t m", p=P))
 
-        def finish_half(t, parts):
+        def store(m0, pair, lo, hi, part, queue):
+            rows = out[P * (2 * pair + lo) : P * (2 * pair + hi), m0 : m0 + QUARTER]
+            queue.dma_start(rows.rearrange("(t p) m -> p t m", p=P), part)
+
+        def finish(m0, pair, parts=1):
             for j in range(parts):
-                lo, hi = BANK * j // parts, BANK * (j + 1) // parts
-                part = res[1][:, t, lo:hi]
-                nc.vector.tensor_tensor(part, y[BANK, t][:, lo:hi], part, ALU.subtract)
-                nc.sync.dma_start(out[P * t : P * (t + 1), BANK + lo : BANK + hi], part)
+                lo, hi = 2 * j // parts, 2 * (j + 1) // parts
+                part = res[m0, pair][:, lo:hi, :]
+                nc.vector.tensor_tensor(part, y[m0, pair][:, lo:hi, :], part, ALU.subtract)
+                store(m0, pair, lo, hi, part, nc.sync)
+
+        minus_y = {}
+
+        def leave_turned(m0):
+            minus_y[m0] = mid.tile([P, 2, QUARTER], F32, name="minus_y%d" % m0, offset=6144 if m0 == 0 else 2048)
+            nc.scalar.activation(minus_y[m0][:], y[m0, 1][:], ACT.Copy, scale=minus_one[:])
+
+        back = {}
+
+        def turn_back(m0, term, start, stop):
+            for mb in range(2):
+                for nb in range(2):
+                    nc.tensor.matmul(
+                        back[m0][:, nb, P * mb : P * (mb + 1)],
+                        term[:, mb, P * nb : P * (nb + 1)],
+                        ident[:],
+                        start=start and (mb, nb) == (0, 0),
+                        stop=stop and (mb, nb) == (1, 1),
+                        is_transpose=True,
+                    )
+
+        def finish_turned(m0):
+            turn_back(m0, minus_y[m0], False, True)
+            done = keep.tile([P, 2, QUARTER], F32, name="done%d" % m0)
+            nc.scalar.activation(done[:], back[m0][:], ACT.Copy, scale=-1.0)
+            store(m0, 1, 0, 2, done[:], nc.scalar)
 
         for k in range(FIRST):
             softplus(k)
             pick(k, 0, M)
             if k in (2, 3):
-                u = k - 2
-                res.append(keep.tile([P, 4, BANK], F32, name="res%d" % u, tag="h%d" % k))
-                nc.sync.dma_start(res[u][:], best[:, BANK * u : BANK * (u + 1)].rearrange("(t p) m -> p t m", p=P))
+                held = keep.tile([P, 4, 2, QUARTER], F32, name="held%d" % k, tag="h%d" % k)
+                for j in range(4):
+                    m0, pair = BANK * (k - 2) + QUARTER * (j // 2), j % 2
+                    if not (pair == 1 and m0 in TURNED):
+                        load_best(m0, pair, held[:, j, :, :])
             if k == 4:
-                cap(0, 0, M)
+                cap_first_pass()
         quant(0, 0, M)
         for m0 in range(BANK, M, QUARTER):
             cap_pair(m0)
@@ -279,8 +336,12 @@ def tile_list_eclass_cost_extraction_kernel(
             h[k] = keep.tile([P, S], F32, name="h%d" % k, tag="h%d" % (k - FIRST))
             for c in range(CHUNKS):
                 raw_cost(k, c)
-        for m0, m1 in ((0, QUARTER), (QUARTER, BANK), (BANK, M)):
-            readout(0, m0, m1)
+        for m0 in range(0, M - QUARTER, QUARTER):
+            readout(0, m0)
+        readout(0, 3 * QUARTER, (0,))
+        for m0 in TURNED:
+            back[m0] = psum.tile([P, 2, QUARTER], F32, name="back", tag="bank")
+            turn_back(m0, best_t[m0], True, False)
         for k in range(FIRST, TILES - 1):
             softplus(k)
             pick(k, 0, M)
@@ -289,7 +350,7 @@ def tile_list_eclass_cost_extraction_kernel(
 
         def product(q):
             quant(1, QUARTER * q, QUARTER * (q + 1))
-            readout(1, QUARTER * q, QUARTER * (q + 1))
+            readout(1, QUARTER * q)
 
         for q in range(4):
             pick(last, QUARTER * q, QUARTER * (q + 1))
@@ -301,12 +362,19 @@ def tile_list_eclass_cost_extraction_kernel(
             cap_rounded(QUARTER * q)
         for q in range(2):
             product(q)
-        for q in range(2, 4):
-            cap_rounded_pair(QUARTER * q)
-            weave_pairs(QUARTER * q)
-        finish_quarter(0)
-        for q in range(2, 4):
-            product(q)
-        finish_quarter(QUARTER)
-        for t in range(4):
-            finish_half(t, 2 if t >= 2 else 1)
+        cap_rounded_pair(2 * QUARTER)
+        weave_pairs(2 * QUARTER)
+        leave_turned(0)
+        cap_rounded_pair(3 * QUARTER)
+        weave_pairs(3 * QUARTER)
+        finish(0, 0)
+        finish_turned(0)
+        product(2)
+        readout(0, 3 * QUARTER, (1,))
+        finish(QUARTER, 0)
+        product(3)
+        finish(QUARTER, 1)
+        for pair in range(2):
+            finish(2 * QUARTER, pair)
+        finish(3 * QUARTER, 0)
+        finish(3 * QUARTER, 1, 2)

@@ -43,16 +43,19 @@ def tile_list_eclass_cost_extraction_kernel(
             return head.tile(shape, dtype, name=name, offset=offset, align_bytes=64)
 
         LATE = 4096
-        LOW = 5440
+        BUD_LATE = 5440
+        BUD_WHOLE = BUD_LATE + 4096
+        TABS = BUD_WHOLE + 8192 - 64
+        LOW = TABS + T - 64
         HIGH = LOW + 16384
 
-        tabs = placed([P, T], U8, "tabs", HIGH + 4096 + 8128)
+        tabs = placed([P, T], U8, "tabs", TABS)
         w4sraw = keep.tile([P, H], U8, name="w4sraw")
         idx = keep.tile([P, S // 16], U16, name="idx")
         nc.sync.dma_start(idx[:], offs)
         nc.scalar.dma_start(tabs[ROWS:P, :].bitcast(I32), tab_scales[0].bitcast(I32))
         nc.sync.dma_start(w4sraw[ROWS:P, :].bitcast(I32), w4_scales[0].bitcast(I32))
-        w4raw = [placed([P, H], U8, "w4raw0", HIGH - H // 2), keep.tile([P, H], U8, name="w4raw1", tag="w4raw1")]
+        w4raw = [placed([P, H], U8, "w4raw0", HIGH - H // 2), keep.tile([P, H], U8, name="w4raw1", tag="w4raw1", align_bytes=64)]
         tabw = keep.tile([P, T], I32, name="tabw", tag="tabw")
         nc.sync.dma_start(tabw[:], tab_words[0].rearrange("p t i -> p (t i)").bitcast(I32))
         for b in range(2):
@@ -82,16 +85,17 @@ def tile_list_eclass_cost_extraction_kernel(
             nc.vector.tensor_copy(stage[96:P, 0:BANK].bitcast(I32), spread[96:P, :].bitcast(I32))
             carry(queue, planes[c][:], stage[:])
 
-        stage0 = keep.tile([P, 2 * BANK], U8, name="stage0")
+        stage0 = keep.tile([P, 2 * BANK], U8, name="stage0", tag="stage0")
         early_scales(0, stage0, nc.scalar)
         stage1 = placed([P, 2 * BANK], U8, "stage1", LATE - 64)
         w4w = [keep.tile([P, H], U8, name="w4w%d" % b, align_bytes=64) for b in range(2)]
-        for k in range(TILES):
-            b, t = divmod(k, 4)
-            nc.gpsimd.tensor_copy(
-                w4w[b][:, 2 * P * t : 2 * P * (t + 1)].rearrange("p (m e) -> p m e", e=2),
-                w4raw[b][:].rearrange("p (m t e) -> p t m e", t=4, e=2)[:, t, :, :],
+
+        def order_w4(b, t0, t1):
+            nc.vector.tensor_copy(
+                w4w[b][:].bitcast(U16).rearrange("p (t m) -> p t m", t=4)[:, t0:t1, :],
+                w4raw[b][:].bitcast(U16).rearrange("p (m t) -> p t m", t=4)[:, t0:t1, :],
             )
+
         early_scales(1, stage1, nc.sync)
         w2raw = {}
 
@@ -102,9 +106,9 @@ def tile_list_eclass_cost_extraction_kernel(
         wgt_sb = placed([P, M], F32, "wgt_sb", HIGH)
         nc.sync.dma_start(wgt_sb[:], wgt)
         load_w2(0)
-        best_early = keep.tile([P, 2, TURN_COLS], F32, name="best_early", tag="w4raw1")
+        best_early = keep.tile([P, 2, TURN_COLS], F32, name="best_early", tag="stage0")
         nc.sync.dma_start(best_early[:], best[2 * P : 4 * P, TURN0 : TURN0 + TURN_COLS].rearrange("(t p) m -> p t m", p=P))
-        vw = [keep.tile([P, 2 * BANK], U32, name="vw_early", align_bytes=64)]
+        vw = [keep.tile([P, BANK], U32, name="vw0", align_bytes=64)[:]]
         vs_late = keep.tile([P, 2 * BANK], U8, name="vs_late", align_bytes=64)
         nc.gpsimd.memset(vs_late[:].bitcast(I32), 0)
         ident = keep.tile([P, P], F32, name="ident")
@@ -120,7 +124,7 @@ def tile_list_eclass_cost_extraction_kernel(
                 out=acc[:],
                 lhsT=w4w[k // 4][:, 2 * P * (k % 4) : 2 * P * (k % 4 + 1)].bitcast(FP4X4),
                 lhsT_scale=planes[k // 4][:, BANK + P * (k % 4) : BANK + P * (k % 4 + 1)],
-                rhs=vw[c // 2][:, BANK * (c % 2) : BANK * (c % 2 + 1)].bitcast(FP8X4),
+                rhs=vw[c].bitcast(FP8X4),
                 rhs_scale=vs[c],
                 start=True,
                 stop=True,
@@ -131,14 +135,22 @@ def tile_list_eclass_cost_extraction_kernel(
             h[k] = keep.tile([P, S], F32, name="h%d" % k, tag="h%d" % k)
         for c in range(CHUNKS):
             cols = idx[:, 32 * c : 32 * (c + 1)]
-            if c >= 2:
-                late = placed([P, BANK], U8, "late%d" % c, LOW - 448 if c == 2 else LATE)
-                nc.vector.tensor_copy(late[:], tabs[:].indirect(cols))
-                carry(nc.sync, vs[c], late[:])
             if c == 2:
+                for d in (2, 3):
+                    late = placed([P, BANK], U8, "late%d" % d, LATE if d == 2 else BUD_LATE - 448)
+                    nc.vector.tensor_copy(late[:], tabs[:].indirect(idx[:, 32 * d : 32 * (d + 1)]))
+                    for q in range(4):
+                        nc.sync.dma_start(vs[d][32 * q : 32 * q + 4, :].bitcast(I32), late[ROWS + 4 * q : ROWS + 4 * q + 4, :].bitcast(I32))
                 load_w2(1)
-                vw.append(placed([P, 2 * BANK], U32, "vw_late", 0))
-            nc.vector.tensor_copy(vw[c // 2][:, BANK * (c % 2) : BANK * (c % 2 + 1)], tabw[:].bitcast(U32).indirect(cols))
+                vw_late = placed([P, 2 * BANK], U32, "vw_late", 0)
+                vw.extend([vw_late[:, 0:BANK], vw_late[:, BANK : 2 * BANK]])
+            if c == 1:
+                vw.append(keep.tile([P, BANK], U32, name="vw1", tag="w4raw1", align_bytes=64)[:])
+            nc.vector.tensor_copy(vw[c], tabw[:].bitcast(U32).indirect(cols))
+            if c == 0:
+                order_w4(0, 0, 2)
+                order_w4(0, 2, 4)
+                order_w4(1, 0, 4)
             for k in range(FIRST):
                 raw_cost(k, c)
 
@@ -157,9 +169,9 @@ def tile_list_eclass_cost_extraction_kernel(
         nc.vector.quantize_mx(out=w2w[:].bitcast(FP8X4), scales=w2s[:], in_=w2bf[:].rearrange("p b c -> p (b c)"))
 
         rows1 = budget[512:1024, :].rearrange("(p i) m -> p i m", i=4)
-        bud_whole = placed([P, 4, BANK], F32, "bud_whole", HIGH + 4096)
+        bud_whole = placed([P, 4, BANK], F32, "bud_whole", BUD_WHOLE)
         nc.sync.dma_start(bud_whole[:], rows1[:, :, 0:BANK])
-        bud_late = placed([P, 2, BANK], F32, "bud_late", HIGH + 4096 + 8128 + T - 64)
+        bud_late = placed([P, 2, BANK], F32, "bud_late", BUD_LATE)
         nc.sync.dma_start(bud_late[:], rows1[:, 2:4, BANK:M])
         bud_early = keep.tile([P, 2, BANK], F32, name="bud_early", tag="w2bf", align_bytes=64)
         nc.sync.dma_start(bud_early[:], rows1[:, 0:2, BANK:M])
@@ -185,7 +197,7 @@ def tile_list_eclass_cost_extraction_kernel(
         bud[0] = placed([P, 4, M], F32, "bud0", LOW)
         nc.sync.dma_start(bud[0][:], budget[0:512, :].rearrange("(p i) m -> p i m", i=4))
 
-        x = [placed([P, 4, M], F32, "x0", HIGH + 4096), keep.tile([P, 4, M], F32, name="x1")]
+        x = [placed([P, 4, M], F32, "x0", LOW - 16384), keep.tile([P, 4, M], F32, name="x1")]
         zw = [keep.tile([P, M], U32, name="zw%d" % b, align_bytes=64) for b in range(2)]
         zs = [keep.tile([P, M], U8, name="zs%d" % b, align_bytes=64) for b in range(2)]
         z = {}

@@ -42,10 +42,13 @@ def tile_list_eclass_cost_extraction_kernel(
         def placed(shape, dtype, name, offset):
             return head.tile(shape, dtype, name=name, offset=offset, align_bytes=64)
 
-        LATE = 4096
-        BUD_LATE = 5440
-        BUD_WHOLE = BUD_LATE + 4096
-        TABS = BUD_WHOLE + 8192 - 64
+        W4_LATE = 3008
+        SPREAD0 = W4_LATE + H - 64
+        SPREAD1 = SPREAD0 + BANK - 64
+        VW_LATE = SPREAD1 + BANK - 64
+        LATE = VW_LATE - 2 * BANK
+        BUD_RAW = VW_LATE + 4096 + 128
+        TABS = BUD_RAW + 12288 - 64
         LOW = TABS + T - 64
         HIGH = LOW + 16384
 
@@ -55,39 +58,40 @@ def tile_list_eclass_cost_extraction_kernel(
         nc.sync.dma_start(idx[:], offs)
         nc.scalar.dma_start(tabs[ROWS:P, :].bitcast(I32), tab_scales[0].bitcast(I32))
         nc.sync.dma_start(w4sraw[ROWS:P, :].bitcast(I32), w4_scales[0].bitcast(I32))
-        w4raw = [placed([P, H], U8, "w4raw0", HIGH - H // 2), keep.tile([P, H], U8, name="w4raw1", tag="w4raw1", align_bytes=64)]
         tabw = keep.tile([P, T], I32, name="tabw", tag="tabw")
-        nc.sync.dma_start(tabw[:], tab_words[0].rearrange("p t i -> p (t i)").bitcast(I32))
-        for b in range(2):
-            nc.sync.dma_start(w4raw[b][:].bitcast(I32), w4_words[0, :, H * b : H * (b + 1)].bitcast(I32))
+        words = tab_words[0].rearrange("p t i -> p (t i)").bitcast(I32)
+        nc.sync.dma_start(tabw[:], words)
+        w4raw = [placed([P, H], U8, "w4raw0", HIGH - H // 2)]
+        nc.sync.dma_start(w4raw[0][:].bitcast(I32), w4_words[0, :, 0:H].bitcast(I32))
         idx2 = keep.tile([P, M // 16], U16, name="idx2")
         nc.sync.dma_start(idx2[:], offs2)
-        gain_sb = keep.tile([P, 2, 4], F32, name="gain_sb")
-        nc.sync.dma_start(gain_sb[:], gain.rearrange("(b p i) -> p b i", b=2, i=4))
-
         nc.vector.memset(tabs[0:ROWS, :].bitcast(I32), 0)
         nc.gpsimd.memset(w4sraw[0:ROWS, :].bitcast(I32), 0)
-        planes = [keep.tile([P, 2 * BANK], U8, name="planes%d" % c, align_bytes=64) for c in range(2)]
-        for c in range(2):
-            nc.gpsimd.memset(planes[c][:].bitcast(I32), 0)
+
+        plane0 = keep.tile([P, BANK + H], U8, name="plane0", align_bytes=64)
+        nc.gpsimd.memset(plane0[:].bitcast(I32), 0)
+        vs_late = keep.tile([P, 3 * BANK], U8, name="vs_late", align_bytes=64)
+        nc.gpsimd.memset(vs_late[:].bitcast(I32), 0)
 
         def carry(queue, plane, rows):
             for q in range(4):
                 queue.dma_start(plane[32 * q : 32 * q + 4, :].bitcast(I32), rows[ROWS + 4 * q : ROWS + 4 * q + 4, :].bitcast(I32))
 
-        def early_scales(c, stage, queue):
-            spread = keep.tile([P, BANK], U8, name="spread%d" % c, tag="spread")
-            nc.vector.tensor_copy(spread[:], tabs[:].indirect(idx[:, 32 * c : 32 * (c + 1)]))
+        stage0 = keep.tile([P, BANK + H], U8, name="stage0", tag="stage0")
+        for b in range(2):
             nc.vector.tensor_copy(
-                stage[:, BANK : 2 * BANK].rearrange("p (t m) -> p t m", t=4),
-                w4sraw[:, BANK * c : BANK * (c + 1)].rearrange("p (m t) -> p t m", t=4),
+                stage0[:, BANK * (b + 1) : BANK * (b + 2)].rearrange("p (t m) -> p t m", t=4),
+                w4sraw[:, BANK * b : BANK * (b + 1)].rearrange("p (m t) -> p t m", t=4),
             )
-            nc.vector.tensor_copy(stage[96:P, 0:BANK].bitcast(I32), spread[96:P, :].bitcast(I32))
-            carry(queue, planes[c][:], stage[:])
-
-        stage0 = keep.tile([P, 2 * BANK], U8, name="stage0", tag="stage0")
-        early_scales(0, stage0, nc.scalar)
-        stage1 = placed([P, 2 * BANK], U8, "stage1", LATE - 64)
+        spread0 = placed([P, BANK], U8, "spread0", SPREAD0)
+        nc.vector.tensor_copy(spread0[:], tabs[:].indirect(idx[:, 0:32]))
+        nc.vector.tensor_copy(stage0[96:P, 0:BANK].bitcast(I32), spread0[96:P, :].bitcast(I32))
+        carry(nc.scalar, plane0[:], stage0[:])
+        w4raw.append(placed([P, H], U8, "w4raw1", W4_LATE))
+        nc.sync.dma_start(w4raw[1][:].bitcast(I32), w4_words[0, :, H : 2 * H].bitcast(I32))
+        spread1 = placed([P, BANK], U8, "spread1", SPREAD1)
+        nc.vector.tensor_copy(spread1[:], tabs[:].indirect(idx[:, 32:64]))
+        carry(nc.sync, vs_late[:, 0:BANK], spread1[:])
         w4w = [keep.tile([P, H], U8, name="w4w%d" % b, align_bytes=64) for b in range(2)]
 
         def order_w4(b, t0, t1):
@@ -96,63 +100,68 @@ def tile_list_eclass_cost_extraction_kernel(
                 w4raw[b][:].bitcast(U16).rearrange("p (m t) -> p t m", t=4)[:, t0:t1, :],
             )
 
-        early_scales(1, stage1, nc.sync)
         w2raw = {}
 
         def load_w2(b):
             w2raw[b] = placed([P, 4, N], F32, "w2raw%d" % b, LOW + 8192 * (1 - b))
             nc.sync.dma_start(w2raw[b][:], w2[512 * b : 512 * (b + 1), :].rearrange("(p j) n -> p j n", j=4))
 
+        vw_first = keep.tile([P, QUARTER], U32, name="vw_first", align_bytes=64)
+        nc.vector.tensor_copy(vw_first[:], tabw[:].bitcast(U32).indirect(idx[:, 0:16]))
+        order_w4(0, 0, 2)
+        order_w4(0, 2, 4)
+        order_w4(1, 0, 4)
+        vw_next = placed([P, QUARTER + BANK], U32, "vw_next", 0)
         wgt_sb = placed([P, M], F32, "wgt_sb", HIGH)
         nc.sync.dma_start(wgt_sb[:], wgt)
+        gain_sb = placed([P, 2, 4], F32, "gain_sb", W4_LATE + 192)
+        nc.sync.dma_start(gain_sb[:], gain.rearrange("(b p i) -> p b i", b=2, i=4))
         load_w2(0)
         best_early = keep.tile([P, 2, TURN_COLS], F32, name="best_early", tag="stage0")
         nc.sync.dma_start(best_early[:], best[2 * P : 4 * P, TURN0 : TURN0 + TURN_COLS].rearrange("(t p) m -> p t m", p=P))
-        vw = [keep.tile([P, BANK], U32, name="vw0", align_bytes=64)[:]]
-        vs_late = keep.tile([P, 2 * BANK], U8, name="vs_late", align_bytes=64)
-        nc.gpsimd.memset(vs_late[:].bitcast(I32), 0)
         ident = keep.tile([P, P], F32, name="ident")
         make_identity(nc, ident[:])
         minus_one = mid.tile([P, 1], F32, name="minus_one", offset=4 * M * TILES)
         nc.gpsimd.memset(minus_one[:], -1.0)
-        vs = [planes[0][:, 0:BANK], planes[1][:, 0:BANK], vs_late[:, 0:BANK], vs_late[:, BANK : 2 * BANK]]
         h = {}
 
-        def raw_cost(k, c):
+        def raw_cost(k, group):
             acc = psum.tile([P, BANK], F32, name="acc", tag="bank")
-            nc.tensor.matmul_mx(
-                out=acc[:],
-                lhsT=w4w[k // 4][:, 2 * P * (k % 4) : 2 * P * (k % 4 + 1)].bitcast(FP4X4),
-                lhsT_scale=planes[k // 4][:, BANK + P * (k % 4) : BANK + P * (k % 4 + 1)],
-                rhs=vw[c].bitcast(FP8X4),
-                rhs_scale=vs[c],
-                start=True,
-                stop=True,
-            )
-            nc.scalar.activation(h[k][:, BANK * c : BANK * (c + 1)], acc[:], ACT.Exp)
+            first, last = group[0][0], group[-1][1]
+            for lo, hi, codes, scales in group:
+                nc.tensor.matmul_mx(
+                    out=acc[:, lo - first : hi - first],
+                    lhsT=w4w[k // 4][:, 2 * P * (k % 4) : 2 * P * (k % 4 + 1)].bitcast(FP4X4),
+                    lhsT_scale=plane0[:, BANK + P * k : BANK + P * (k + 1)],
+                    rhs=codes.bitcast(FP8X4),
+                    rhs_scale=scales,
+                    start=True,
+                    stop=True,
+                )
+            nc.scalar.activation(h[k][:, first:last], acc[:, 0 : last - first], ACT.Exp)
 
         for k in range(FIRST):
             h[k] = keep.tile([P, S], F32, name="h%d" % k, tag="h%d" % k)
-        for c in range(CHUNKS):
-            cols = idx[:, 32 * c : 32 * (c + 1)]
-            if c == 2:
-                for d in (2, 3):
-                    late = placed([P, BANK], U8, "late%d" % d, LATE if d == 2 else BUD_LATE - 448)
-                    nc.vector.tensor_copy(late[:], tabs[:].indirect(idx[:, 32 * d : 32 * (d + 1)]))
-                    for q in range(4):
-                        nc.sync.dma_start(vs[d][32 * q : 32 * q + 4, :].bitcast(I32), late[ROWS + 4 * q : ROWS + 4 * q + 4, :].bitcast(I32))
+        late = placed([P, 2 * BANK], U8, "late", LATE)
+        vw_late = placed([P, 2 * BANK], U32, "vw_late", VW_LATE)
+        runs = [
+            (0, QUARTER, vw_first[:], plane0[:, 0:QUARTER]),
+            (QUARTER, BANK, vw_next[:, 0:QUARTER], plane0[:, QUARTER:BANK]),
+            (BANK, 2 * BANK, vw_next[:, QUARTER : QUARTER + BANK], vs_late[:, 0:BANK]),
+            (2 * BANK, 3 * BANK, vw_late[:, 0:BANK], vs_late[:, BANK : 2 * BANK]),
+            (3 * BANK, 4 * BANK, vw_late[:, BANK : 2 * BANK], vs_late[:, 2 * BANK : 3 * BANK]),
+        ]
+        for j, (lo, hi, codes, scales) in enumerate(runs):
+            if j == 3:
+                for d in range(2):
+                    part = late[:, BANK * d : BANK * (d + 1)]
+                    nc.vector.tensor_copy(part, tabs[:].indirect(idx[:, 64 + 32 * d : 96 + 32 * d]))
+                    carry(nc.sync, vs_late[:, BANK * (d + 1) : BANK * (d + 2)], part)
                 load_w2(1)
-                vw_late = placed([P, 2 * BANK], U32, "vw_late", 0)
-                vw.extend([vw_late[:, 0:BANK], vw_late[:, BANK : 2 * BANK]])
-            if c == 1:
-                vw.append(keep.tile([P, BANK], U32, name="vw1", tag="w4raw1", align_bytes=64)[:])
-            nc.vector.tensor_copy(vw[c], tabw[:].bitcast(U32).indirect(cols))
-            if c == 0:
-                order_w4(0, 0, 2)
-                order_w4(0, 2, 4)
-                order_w4(1, 0, 4)
+            if j > 0:
+                nc.vector.tensor_copy(codes, tabw[:].bitcast(U32).indirect(idx[:, lo // 16 : hi // 16]))
             for k in range(FIRST):
-                raw_cost(k, c)
+                raw_cost(k, runs[j : j + 1])
 
         w2bf = keep.tile([P, 2, N * 4], BF16, name="w2bf", tag="w2bf", align_bytes=64)
         w2w = keep.tile([P, 2 * N], U32, name="w2w", align_bytes=64)
@@ -169,21 +178,22 @@ def tile_list_eclass_cost_extraction_kernel(
         nc.vector.quantize_mx(out=w2w[:].bitcast(FP8X4), scales=w2s[:], in_=w2bf[:].rearrange("p b c -> p (b c)"))
 
         rows1 = budget[512:1024, :].rearrange("(p i) m -> p i m", i=4)
-        bud_whole = placed([P, 4, BANK], F32, "bud_whole", BUD_WHOLE)
-        nc.sync.dma_start(bud_whole[:], rows1[:, :, 0:BANK])
-        bud_late = placed([P, 2, BANK], F32, "bud_late", BUD_LATE)
-        nc.sync.dma_start(bud_late[:], rows1[:, 2:4, BANK:M])
+        bud_raw = placed([P, 6, BANK], F32, "bud_raw", BUD_RAW)
+        bud_whole = bud_raw[:, 0:4, :]
+        nc.sync.dma_start(bud_whole, rows1[:, :, 0:BANK])
+        bud_late = bud_raw[:, 4:6, :]
+        nc.sync.dma_start(bud_late, rows1[:, 2:4, BANK:M])
         bud_early = keep.tile([P, 2, BANK], F32, name="bud_early", tag="w2bf", align_bytes=64)
         nc.sync.dma_start(bud_early[:], rows1[:, 0:2, BANK:M])
         bud = {}
         bud_bf = keep.tile([P, 3 * M], BF16, name="bud_bf", tag="tabw")
         nc.vector.tensor_copy(
             bud_bf[:, 0 : 2 * M].rearrange("p (c i t) -> p c t i", i=4, t=4),
-            bud_whole[:].rearrange("p t (c i) -> p c t i", i=4),
+            bud_whole.rearrange("p t (c i) -> p c t i", i=4),
         )
         nc.vector.tensor_copy(
             bud_bf[:, 2 * M : 3 * M].rearrange("p (c i t) -> p c t i", i=4, t=2),
-            bud_late[:].rearrange("p t (c i) -> p c t i", i=4),
+            bud_late.rearrange("p t (c i) -> p c t i", i=4),
         )
         best_t = {}
         for m0 in TURNED:
@@ -346,8 +356,8 @@ def tile_list_eclass_cost_extraction_kernel(
             cap_pair(m0)
         for k in range(FIRST, TILES):
             h[k] = keep.tile([P, S], F32, name="h%d" % k, tag="h%d" % (k - FIRST))
-            for c in range(CHUNKS):
-                raw_cost(k, c)
+            for group in (runs[0:2], runs[2:3], runs[3:4], runs[4:5]):
+                raw_cost(k, group)
         for m0 in range(0, M - QUARTER, QUARTER):
             readout(0, m0)
         readout(0, 3 * QUARTER, (0,))

@@ -66,6 +66,10 @@ def tile_list_eclass_cost_extraction_kernel(
         idx2 = keep.tile([P, M // 16], U16, name="idx2")
         nc.sync.dma_start(idx2[:], offs2)
         nc.vector.memset(tabs[0:ROWS, :].bitcast(I32), 0)
+        ident = keep.tile([P, P], F32, name="ident")
+        nc.gpsimd.memset(ident[:], 0.0)
+        minus_one = mid.tile([P, 1], F32, name="minus_one", offset=4 * M * TILES)
+        nc.scalar.activation(minus_one[:], ident[:, 0:1], ACT.Copy, scale=0.0, bias=-1.0)
         nc.gpsimd.memset(w4sraw[0:ROWS, :].bitcast(I32), 0)
 
         plane0 = keep.tile([P, BANK + H], U8, name="plane0", align_bytes=64)
@@ -94,8 +98,8 @@ def tile_list_eclass_cost_extraction_kernel(
         carry(nc.sync, vs_late[:, 0:BANK], spread1[:])
         w4w = [keep.tile([P, H], U8, name="w4w%d" % b, align_bytes=64) for b in range(2)]
 
-        def order_w4(b, t0, t1):
-            nc.vector.tensor_copy(
+        def order_w4(b, t0, t1, move=nc.vector.tensor_copy):
+            move(
                 w4w[b][:].bitcast(U16).rearrange("p (t m) -> p t m", t=4)[:, t0:t1, :],
                 w4raw[b][:].bitcast(U16).rearrange("p (m t) -> p t m", t=4)[:, t0:t1, :],
             )
@@ -108,7 +112,7 @@ def tile_list_eclass_cost_extraction_kernel(
 
         vw_first = keep.tile([P, QUARTER], U32, name="vw_first", align_bytes=64)
         nc.vector.tensor_copy(vw_first[:], tabw[:].bitcast(U32).indirect(idx[:, 0:16]))
-        order_w4(0, 0, 2)
+        order_w4(0, 0, 2, nc.scalar.copy)
         order_w4(0, 2, 4)
         order_w4(1, 0, 4)
         vw_next = placed([P, QUARTER + BANK], U32, "vw_next", 0)
@@ -119,10 +123,7 @@ def tile_list_eclass_cost_extraction_kernel(
         load_w2(0)
         best_early = keep.tile([P, 2, TURN_COLS], F32, name="best_early", tag="stage0")
         nc.sync.dma_start(best_early[:], best[2 * P : 4 * P, TURN0 : TURN0 + TURN_COLS].rearrange("(t p) m -> p t m", p=P))
-        ident = keep.tile([P, P], F32, name="ident")
-        make_identity(nc, ident[:])
-        minus_one = mid.tile([P, 1], F32, name="minus_one", offset=4 * M * TILES)
-        nc.gpsimd.memset(minus_one[:], -1.0)
+        make_identity(nc, ident[:], nomemset=True)
         h = {}
 
         def raw_cost(k, group):
@@ -166,6 +167,7 @@ def tile_list_eclass_cost_extraction_kernel(
         w2bf = keep.tile([P, 2, N * 4], BF16, name="w2bf", tag="w2bf", align_bytes=64)
         w2w = keep.tile([P, 2 * N], U32, name="w2w", align_bytes=64)
         w2s = keep.tile([P, 2 * N], U8, name="w2s", align_bytes=64)
+        nc.gpsimd.memset(w2s[:, 0:N].bitcast(I32), 0)
         wg = []
         for k in range(TILES):
             wg.append(mid.tile([P, M], F32, name="wg%d" % k, offset=4 * M * k))
@@ -285,7 +287,8 @@ def tile_list_eclass_cost_extraction_kernel(
                     else:
                         still = slice(N * b + P * (2 * pair + j), N * b + P * (2 * pair + j + 1))
                         moving = slice(m0, m0 + QUARTER)
-                        lhs, lhs_s, rhs, rhs_s = w2w[:, still], w2s[:, still], zw[b][:, moving], zs[b][:, moving]
+                        plane = w2s_held if b == 0 and m0 > 0 else w2s
+                        lhs, lhs_s, rhs, rhs_s = w2w[:, still], plane[:, still], zw[b][:, moving], zs[b][:, moving]
                     nc.tensor.matmul_mx(
                         out=y[m0, pair][:, j, :],
                         lhsT=lhs.bitcast(FP8X4),
@@ -358,9 +361,7 @@ def tile_list_eclass_cost_extraction_kernel(
             h[k] = keep.tile([P, S], F32, name="h%d" % k, tag="h%d" % (k - FIRST))
             for group in (runs[0:2], runs[2:3], runs[3:4], runs[4:5]):
                 raw_cost(k, group)
-        for m0 in range(0, M - QUARTER, QUARTER):
-            readout(0, m0)
-        readout(0, 3 * QUARTER, (0,))
+        readout(0, 0)
         for m0 in TURNED:
             back[m0] = psum.tile([P, 2, QUARTER], F32, name="back", tag="bank")
             turn_back(m0, best_t[m0], True, False)
@@ -369,6 +370,11 @@ def tile_list_eclass_cost_extraction_kernel(
             pick(k, 0, M)
         last = TILES - 1
         softplus(last)
+        w2s_held = mid.tile([P, N], U8, name="w2s_held", align_bytes=64, offset=4 * M * (TILES - 2))
+        nc.scalar.copy(w2s_held[:].bitcast(U32), w2s[:, 0:N].bitcast(U32))
+        readout(0, QUARTER)
+        readout(0, 2 * QUARTER)
+        readout(0, 3 * QUARTER, (0,))
 
         def product(q):
             quant(1, QUARTER * q, QUARTER * (q + 1))

@@ -206,7 +206,7 @@ def tile_list_eclass_cost_extraction_kernel(
                     nc.tensor.transpose(turn[:, mb, P * nb : P * (nb + 1)], best_early[:, nb, lo : lo + P], ident[:])
             best_t[m0] = keep.tile([P, 2, QUARTER], F32, name="best_t%d" % m0)
             nc.vector.tensor_copy(best_t[m0][:], turn[:])
-        bud[0] = placed([P, 4, M], F32, "bud0", LOW)
+        bud[0] = placed([P, 4, M], F32, "bud0", HIGH + 4 * M - 64)
         nc.sync.dma_start(bud[0][:], budget[0:512, :].rearrange("(p i) m -> p i m", i=4))
 
         x = [placed([P, 4, M], F32, "x0", LOW - 16384), keep.tile([P, 4, M], F32, name="x1")]
@@ -343,15 +343,13 @@ def tile_list_eclass_cost_extraction_kernel(
             nc.scalar.activation(done[:], back[m0][:], ACT.Copy, scale=-1.0)
             store(m0, 1, 0, 2, done[:], nc.scalar)
 
+        for j in range(TILES):
+            m0, pair = QUARTER * (j // 2), j % 2
+            if not (pair == 1 and m0 in TURNED):
+                load_best(m0, pair, placed([P, 2, QUARTER], F32, "best%d" % j, LOW + 8 * QUARTER * j)[:])
         for k in range(FIRST):
             softplus(k)
             pick(k, 0, M)
-            if k in (2, 3):
-                held = keep.tile([P, 4, 2, QUARTER], F32, name="held%d" % k, tag="h%d" % k)
-                for j in range(4):
-                    m0, pair = BANK * (k - 2) + QUARTER * (j // 2), j % 2
-                    if not (pair == 1 and m0 in TURNED):
-                        load_best(m0, pair, held[:, j, :, :])
             if k == 4:
                 cap_first_pass()
         quant(0, 0, M)

@@ -24,9 +24,8 @@ CHUNKS = S // BANK
 TILES = H // P
 FIRST = 6
 ROWS = P - 16
-TURNED = (0,)
-TURN0 = 0
-TURN_COLS = QUARTER
+Y_BANK = ((0, 1), (2, 3), (4, 5), (6, 7))
+TURNED = (0, QUARTER)
 
 
 def tile_list_eclass_cost_extraction_kernel(
@@ -35,7 +34,7 @@ def tile_list_eclass_cost_extraction_kernel(
     nc = tc.nc
     with ExitStack() as ctx:
         keep = ctx.enter_context(tc.tile_pool(name="keep", bufs=1))
-        psum = ctx.enter_context(tc.psum_pool(name="psum", bufs=8))
+        psum = ctx.enter_context(tc.psum_pool(name="psum", bufs=1))
         head = ctx.enter_context(tc.tile_pool(name="head", bufs=1))
         mid = ctx.enter_context(tc.tile_pool(name="mid", bufs=1))
 
@@ -48,7 +47,7 @@ def tile_list_eclass_cost_extraction_kernel(
         VW_LATE = SPREAD1 + BANK - 64
         LATE = VW_LATE - 2 * BANK
         BUD_RAW = VW_LATE + 4096 + 128
-        TABS = BUD_RAW + 12288 - 64
+        TABS = BUD_RAW + 16384 - 64
         LOW = TABS + T - 64
         HIGH = LOW + 16384
 
@@ -68,8 +67,11 @@ def tile_list_eclass_cost_extraction_kernel(
         nc.vector.memset(tabs[0:ROWS, :].bitcast(I32), 0)
         ident = keep.tile([P, P], F32, name="ident")
         nc.gpsimd.memset(ident[:], 0.0)
-        minus_one = mid.tile([P, 1], F32, name="minus_one", offset=4 * M * TILES)
-        nc.scalar.activation(minus_one[:], ident[:, 0:1], ACT.Copy, scale=0.0, bias=-1.0)
+        SIGNS = 4 * M * TILES
+        minus_one = {}
+        for m0 in TURNED:
+            minus_one[m0] = mid.tile([P, 1], F32, name="minus_one%d" % m0, offset=SIGNS + 4 * m0)
+            nc.scalar.activation(minus_one[m0][:], ident[:, 0:1], ACT.Copy, scale=0.0, bias=-1.0)
         nc.gpsimd.memset(w4sraw[0:ROWS, :].bitcast(I32), 0)
 
         plane0 = keep.tile([P, BANK + H], U8, name="plane0", align_bytes=64)
@@ -81,7 +83,7 @@ def tile_list_eclass_cost_extraction_kernel(
             for q in range(4):
                 queue.dma_start(plane[32 * q : 32 * q + 4, :].bitcast(I32), rows[ROWS + 4 * q : ROWS + 4 * q + 4, :].bitcast(I32))
 
-        stage0 = keep.tile([P, BANK + H], U8, name="stage0", tag="stage0")
+        stage0 = keep.tile([P, BANK + H], U8, name="stage0")
         for b in range(2):
             nc.vector.tensor_copy(
                 stage0[:, BANK * (b + 1) : BANK * (b + 2)].rearrange("p (t m) -> p t m", t=4),
@@ -113,7 +115,7 @@ def tile_list_eclass_cost_extraction_kernel(
         vw_first = keep.tile([P, QUARTER], U32, name="vw_first", align_bytes=64)
         nc.vector.tensor_copy(vw_first[:], tabw[:].bitcast(U32).indirect(idx[:, 0:16]))
         order_w4(0, 0, 2, nc.scalar.copy)
-        order_w4(0, 2, 4)
+        order_w4(0, 2, 4, nc.scalar.copy)
         order_w4(1, 0, 4)
         vw_next = placed([P, QUARTER + BANK], U32, "vw_next", 0)
         wgt_sb = placed([P, M], F32, "wgt_sb", HIGH)
@@ -121,13 +123,17 @@ def tile_list_eclass_cost_extraction_kernel(
         gain_sb = placed([P, 2, 4], F32, "gain_sb", W4_LATE + 192)
         nc.sync.dma_start(gain_sb[:], gain.rearrange("(b p i) -> p b i", b=2, i=4))
         load_w2(0)
-        best_early = keep.tile([P, 2, TURN_COLS], F32, name="best_early", tag="stage0")
-        nc.sync.dma_start(best_early[:], best[2 * P : 4 * P, TURN0 : TURN0 + TURN_COLS].rearrange("(t p) m -> p t m", p=P))
         make_identity(nc, ident[:], nomemset=True)
         h = {}
 
+        sums = []
+
+        def bank(j, shape, name):
+            return psum.tile(shape, F32, name=name, tag="bank%d" % j)
+
         def raw_cost(k, group):
-            acc = psum.tile([P, BANK], F32, name="acc", tag="bank")
+            acc = bank(len(sums) % 8, [P, BANK], "acc")
+            sums.append(acc)
             first, last = group[0][0], group[-1][1]
             for lo, hi, codes, scales in group:
                 nc.tensor.matmul_mx(
@@ -168,10 +174,14 @@ def tile_list_eclass_cost_extraction_kernel(
         w2w = keep.tile([P, 2 * N], U32, name="w2w", align_bytes=64)
         w2s = keep.tile([P, 2 * N], U8, name="w2s", align_bytes=64)
         nc.gpsimd.memset(w2s[:, 0:N].bitcast(I32), 0)
-        wg = []
+        wg = {}
         for k in range(TILES):
-            wg.append(mid.tile([P, M], F32, name="wg%d" % k, offset=4 * M * k))
-            nc.vector.tensor_scalar(wg[k][:], wgt_sb[:], gain_sb[:, k // 4, k % 4 : k % 4 + 1], None, ALU.mult)
+            width = M
+            for m0 in range(0, M, width):
+                wg[k, m0] = mid.tile([P, width], F32, name="wg%d_%d" % (k, m0), offset=4 * M * k + 4 * m0)
+                nc.vector.tensor_scalar(
+                    wg[k, m0][:], wgt_sb[:, m0 : m0 + width], gain_sb[:, k // 4, k % 4 : k % 4 + 1], None, ALU.mult
+                )
         for b in range(2):
             nc.vector.tensor_copy(
                 w2bf[:, b, :].rearrange("p (c i t) -> p c t i", i=4, t=4),
@@ -180,38 +190,32 @@ def tile_list_eclass_cost_extraction_kernel(
         nc.vector.quantize_mx(out=w2w[:].bitcast(FP8X4), scales=w2s[:], in_=w2bf[:].rearrange("p b c -> p (b c)"))
 
         rows1 = budget[512:1024, :].rearrange("(p i) m -> p i m", i=4)
-        bud_raw = placed([P, 6, BANK], F32, "bud_raw", BUD_RAW)
-        bud_whole = bud_raw[:, 0:4, :]
-        nc.sync.dma_start(bud_whole, rows1[:, :, 0:BANK])
-        bud_late = bud_raw[:, 4:6, :]
-        nc.sync.dma_start(bud_late, rows1[:, 2:4, BANK:M])
-        bud_early = keep.tile([P, 2, BANK], F32, name="bud_early", tag="w2bf", align_bytes=64)
-        nc.sync.dma_start(bud_early[:], rows1[:, 0:2, BANK:M])
+        bud_raw = placed([P, 2, 4, BANK], F32, "bud_raw", BUD_RAW)
         bud = {}
-        bud_bf = keep.tile([P, 3 * M], BF16, name="bud_bf", tag="tabw")
-        nc.vector.tensor_copy(
-            bud_bf[:, 0 : 2 * M].rearrange("p (c i t) -> p c t i", i=4, t=4),
-            bud_whole.rearrange("p t (c i) -> p c t i", i=4),
-        )
-        nc.vector.tensor_copy(
-            bud_bf[:, 2 * M : 3 * M].rearrange("p (c i t) -> p c t i", i=4, t=2),
-            bud_late.rearrange("p t (c i) -> p c t i", i=4),
-        )
+        bud_bf = keep.tile([P, 4 * M], BF16, name="bud_bf", tag="tabw")
+        for half in range(2):
+            nc.sync.dma_start(bud_raw[:, half, :, :], rows1[:, :, BANK * half : BANK * (half + 1)])
+        for half in range(2):
+            nc.vector.tensor_copy(
+                bud_bf[:, 2 * M * half : 2 * M * (half + 1)].rearrange("p (c i t) -> p c t i", i=4, t=4),
+                bud_raw[:, half, :, :].rearrange("p t (c i) -> p c t i", i=4),
+            )
         best_t = {}
-        for m0 in TURNED:
-            turn = psum.tile([P, 2, QUARTER], F32, name="turn", tag="bank")
+
+        def turn_best(m0, j):
+            turn = bank(j, [P, 2, QUARTER], "turn")
             for mb in range(2):
                 for nb in range(2):
-                    lo = m0 - TURN0 + P * mb
-                    nc.tensor.transpose(turn[:, mb, P * nb : P * (nb + 1)], best_early[:, nb, lo : lo + P], ident[:])
-            best_t[m0] = keep.tile([P, 2, QUARTER], F32, name="best_t%d" % m0)
-            nc.vector.tensor_copy(best_t[m0][:], turn[:])
+                    nc.tensor.transpose(turn[:, mb, P * nb : P * (nb + 1)], res[m0, 1][:, nb, P * mb : P * (mb + 1)], ident[:])
+            return turn
+
         bud[0] = placed([P, 4, M], F32, "bud0", HIGH + 4 * M - 64)
         nc.sync.dma_start(bud[0][:], budget[0:512, :].rearrange("(p i) m -> p i m", i=4))
 
         x = [placed([P, 4, M], F32, "x0", LOW - 16384), keep.tile([P, 4, M], F32, name="x1")]
-        zw = [keep.tile([P, M], U32, name="zw%d" % b, align_bytes=64) for b in range(2)]
+        zw0 = keep.tile([P, M], U32, name="zw0", align_bytes=64)
         zs = [keep.tile([P, M], U8, name="zs%d" % b, align_bytes=64) for b in range(2)]
+        zw = {(0, m0): zw0[:, m0 : m0 + QUARTER] for m0 in range(0, M, QUARTER)}
         z = {}
 
         def softplus(k):
@@ -219,7 +223,7 @@ def tile_list_eclass_cost_extraction_kernel(
 
         def pick(k, m0, m1):
             nc.vector.tensor_tensor(
-                x[k // 4][:, k % 4, m0:m1], h[k][:].indirect(idx2[:, m0 // 16 : m1 // 16]), wg[k][:, m0:m1], ALU.mult
+                x[k // 4][:, k % 4, m0:m1], h[k][:].indirect(idx2[:, m0 // 16 : m1 // 16]), wg[k, 0][:, m0:m1], ALU.mult
             )
 
         def cap_first_pass():
@@ -231,64 +235,47 @@ def tile_list_eclass_cost_extraction_kernel(
                 ALU.min,
             )
 
-        def weave(m0):
-            z[1, m0] = keep.tile([P, 4 * QUARTER], BF16, name="z1_%d" % m0, align_bytes=64)
-            nc.scalar.copy(
-                z[1, m0][:].rearrange("p (c i t) -> p c t i", i=4, t=4),
-                x[1][:, :, m0 : m0 + QUARTER].rearrange("p t (c i) -> p c t i", i=4),
-            )
-
-        def cap_rounded(m0):
-            nc.vector.tensor_tensor(z[1, m0][:], z[1, m0][:], bud_bf[:, 4 * m0 : 4 * (m0 + QUARTER)], ALU.min)
-
         pairs = {}
 
-        def cap_pair(m0):
-            pairs[m0] = mid.tile([P, 2, 2 * QUARTER], BF16, name="pairs%d" % m0, offset=6144 if m0 == BANK else 2048)
-            cols = slice(m0, m0 + QUARTER)
+        def round_pair(m0, u, move):
+            if u == 0:
+                pairs[m0] = mid.tile([P, 2, 2 * QUARTER], BF16, name="pairs%d" % m0, offset=8 * m0)
+            move(
+                pairs[m0][:, u, :].rearrange("p (c i t) -> p c t i", i=4, t=2),
+                x[1][:, 2 * u : 2 * u + 2, m0 : m0 + QUARTER].rearrange("p t (c i) -> p c t i", i=4),
+            )
+
+        def cap_woven(m0):
+            z[1, m0] = keep.tile([P, 4 * QUARTER], BF16, name="z1_%d" % m0, tag="z1_%d" % m0 if m0 < M - QUARTER else "minus_y0", align_bytes=64)
             nc.vector.tensor_tensor(
-                pairs[m0][:, 0, :].rearrange("p (c i t) -> p c t i", i=4, t=2),
-                x[1][:, 0:2, cols].rearrange("p t (c i) -> p c t i", i=4),
-                bud_early[:, :, m0 - BANK : m0 - BANK + QUARTER].rearrange("p t (c i) -> p c t i", i=4),
+                z[1, m0][:].rearrange("p (c u t) -> p c u t", u=2, t=2),
+                pairs[m0][:].rearrange("p u (c t) -> p c u t", t=2),
+                bud_bf[:, 4 * m0 : 4 * (m0 + QUARTER)].rearrange("p (c u t) -> p c u t", u=2, t=2),
                 ALU.min,
             )
 
-        def round_pair(m0):
-            nc.scalar.copy(
-                pairs[m0][:, 1, :].rearrange("p (c i t) -> p c t i", i=4, t=2),
-                x[1][:, 2:4, m0 : m0 + QUARTER].rearrange("p t (c i) -> p c t i", i=4),
-            )
-
-        def cap_rounded_pair(m0):
-            lo = 2 * M + 2 * (m0 - BANK)
-            nc.vector.tensor_tensor(pairs[m0][:, 1, :], pairs[m0][:, 1, :], bud_bf[:, lo : lo + 2 * QUARTER], ALU.min)
-
-        def weave_pairs(m0):
-            z[1, m0] = mid.tile([P, 4 * QUARTER], BF16, name="z1_%d" % m0, align_bytes=64, offset=4 * M * TILES + 8 * (M - QUARTER - m0))
-            nc.scalar.copy(
-                z[1, m0][:].bitcast(U32).rearrange("p (c i u) -> p c u i", i=4, u=2),
-                pairs[m0][:].rearrange("p u c -> p (u c)").bitcast(U32).rearrange("p (u c i) -> p c u i", u=2, i=4),
-            )
-
-        def quant(b, m0, m1):
-            nc.vector.quantize_mx(out=zw[b][:, m0:m1].bitcast(FP8X4), scales=zs[b][:, m0:m1], in_=z[b, m0][:])
+        def quant(m0):
+            offset = SIGNS + 4 * max(QUARTER, M - QUARTER - m0)
+            zw[1, m0] = mid.tile([P, QUARTER], U32, name="zw1_%d" % m0, align_bytes=64, offset=offset)[:]
+            nc.vector.quantize_mx(out=zw[1, m0].bitcast(FP8X4), scales=zs[1][:, m0 : m0 + QUARTER], in_=z[1, m0][:])
 
         y = {}
 
         def readout(b, m0, which=(0, 1)):
             for pair in which:
                 if b == 0:
-                    y[m0, pair] = psum.tile([P, 2, QUARTER], F32, name="y", tag="bank")
+                    y[m0, pair] = bank(Y_BANK[m0 // QUARTER][pair], [P, 2, QUARTER], "y")
+                if b == 0 and m0 in (QUARTER, BANK):
+                    zplane = held[:, m0 - QUARTER : m0]
+                else:
+                    zplane = zs[b][:, m0 : m0 + QUARTER]
                 for j in range(2):
                     if pair == 1 and m0 in TURNED:
-                        still = slice(m0 + P * j, m0 + P * (j + 1))
                         moving = slice(N * b + QUARTER, N * (b + 1))
-                        lhs, lhs_s, rhs, rhs_s = zw[b][:, still], zs[b][:, still], w2w[:, moving], w2s[:, moving]
+                        lhs, lhs_s, rhs, rhs_s = zw[b, m0][:, P * j : P * (j + 1)], zplane[:, P * j : P * (j + 1)], w2w[:, moving], w2s[:, moving]
                     else:
                         still = slice(N * b + P * (2 * pair + j), N * b + P * (2 * pair + j + 1))
-                        moving = slice(m0, m0 + QUARTER)
-                        plane = w2s_held if b == 0 and m0 > 0 else w2s
-                        lhs, lhs_s, rhs, rhs_s = w2w[:, still], plane[:, still], zw[b][:, moving], zs[b][:, moving]
+                        lhs, lhs_s, rhs, rhs_s = w2w[:, still], w2s[:, still], zw[b, m0], zplane
                     nc.tensor.matmul_mx(
                         out=y[m0, pair][:, j, :],
                         lhsT=lhs.bitcast(FP8X4),
@@ -320,8 +307,8 @@ def tile_list_eclass_cost_extraction_kernel(
         minus_y = {}
 
         def leave_turned(m0):
-            minus_y[m0] = mid.tile([P, 2, QUARTER], F32, name="minus_y%d" % m0, offset=6144 if m0 == 0 else 2048)
-            nc.scalar.activation(minus_y[m0][:], y[m0, 1][:], ACT.Copy, scale=minus_one[:])
+            minus_y[m0] = keep.tile([P, 2, QUARTER], F32, name="minus_y%d" % m0, tag="minus_y%d" % m0, align_bytes=64)
+            nc.scalar.activation(minus_y[m0][:], y[m0, 1][:], ACT.Copy, scale=minus_one[m0][:])
 
         back = {}
 
@@ -339,68 +326,72 @@ def tile_list_eclass_cost_extraction_kernel(
 
         def finish_turned(m0):
             turn_back(m0, minus_y[m0], False, True)
-            done = keep.tile([P, 2, QUARTER], F32, name="done%d" % m0)
-            nc.scalar.activation(done[:], back[m0][:], ACT.Copy, scale=-1.0)
-            store(m0, 1, 0, 2, done[:], nc.scalar)
+            res[m0, 1] = keep.tile([P, 2, QUARTER], F32, name="done%d" % m0)[:]
+            nc.scalar.activation(res[m0, 1], back[m0][:], ACT.Copy, scale=-1.0)
+            store(m0, 1, 0, 2, res[m0, 1], nc.scalar)
 
         for j in range(TILES):
             m0, pair = QUARTER * (j // 2), j % 2
-            if not (pair == 1 and m0 in TURNED):
-                load_best(m0, pair, placed([P, 2, QUARTER], F32, "best%d" % j, LOW + 8 * QUARTER * j)[:])
+            load_best(m0, pair, placed([P, 2, QUARTER], F32, "best%d" % j, LOW + 8 * QUARTER * j)[:])
         for k in range(FIRST):
             softplus(k)
             pick(k, 0, M)
             if k == 4:
                 cap_first_pass()
-        quant(0, 0, M)
-        for m0 in range(BANK, M, QUARTER):
-            cap_pair(m0)
+        nc.vector.quantize_mx(out=zw0[:].bitcast(FP8X4), scales=zs[0][:], in_=z[0, 0][:])
+        for m0 in range(0, M, QUARTER):
+            round_pair(m0, 0, nc.vector.tensor_copy)
         for k in range(FIRST, TILES):
             h[k] = keep.tile([P, S], F32, name="h%d" % k, tag="h%d" % (k - FIRST))
             for group in (runs[0:2], runs[2:3], runs[3:4], runs[4:5]):
                 raw_cost(k, group)
         readout(0, 0)
-        for m0 in TURNED:
-            back[m0] = psum.tile([P, 2, QUARTER], F32, name="back", tag="bank")
-            turn_back(m0, best_t[m0], True, False)
+        turn = {m0: turn_best(m0, 6 + m0 // QUARTER) for m0 in TURNED}
         for k in range(FIRST, TILES - 1):
             softplus(k)
             pick(k, 0, M)
         last = TILES - 1
         softplus(last)
-        w2s_held = mid.tile([P, N], U8, name="w2s_held", align_bytes=64, offset=4 * M * (TILES - 2))
-        nc.scalar.copy(w2s_held[:].bitcast(U32), w2s[:, 0:N].bitcast(U32))
-        readout(0, QUARTER)
-        readout(0, 2 * QUARTER)
-        readout(0, 3 * QUARTER, (0,))
 
-        def product(q):
-            quant(1, QUARTER * q, QUARTER * (q + 1))
-            readout(1, QUARTER * q)
+        held = mid.tile([P, BANK], U8, name="held", align_bytes=64, offset=4 * M * (TILES - 2))
+        nc.scalar.copy(held[:].bitcast(U32), zs[0][:, QUARTER : M - QUARTER].bitcast(U32))
+
+        def open_back(m0, tile):
+            best_t[m0] = tile
+            nc.scalar.copy(best_t[m0][:], turn[m0][:])
+            back[m0] = bank(6 + m0 // QUARTER, [P, 2, QUARTER], "back")
+            turn_back(m0, best_t[m0], True, False)
+
+        readout(0, QUARTER)
+        open_back(0, mid.tile([P, 2, QUARTER], F32, name="best_t0", offset=4 * M * (TILES - 2) + M))
+        readout(0, 2 * QUARTER)
+
+        def product(q, which=(0, 1)):
+            quant(QUARTER * q)
+            readout(1, QUARTER * q, which)
 
         for q in range(4):
-            pick(last, QUARTER * q, QUARTER * (q + 1))
-            if q < 2:
-                weave(QUARTER * q)
-            else:
-                round_pair(QUARTER * q)
-        for q in range(2):
-            cap_rounded(QUARTER * q)
-        for q in range(2):
-            product(q)
-        cap_rounded_pair(2 * QUARTER)
-        weave_pairs(2 * QUARTER)
+            if q % 2 == 0:
+                pick(last, QUARTER * q, QUARTER * (q + 2))
+            round_pair(QUARTER * q, 1, nc.scalar.copy)
+            if q == 1:
+                open_back(QUARTER, keep.tile([P, 2, QUARTER], F32, name="best_t1", tag="h0"))
+        cap_woven(0)
+        cap_woven(QUARTER)
+        product(0, (1, 0))
+        product(1, (1, 0))
+        cap_woven(2 * QUARTER)
         leave_turned(0)
-        cap_rounded_pair(3 * QUARTER)
-        weave_pairs(3 * QUARTER)
+        leave_turned(QUARTER)
         finish(0, 0)
         finish_turned(0)
-        product(2)
-        readout(0, 3 * QUARTER, (1,))
         finish(QUARTER, 0)
+        finish_turned(QUARTER)
+        product(2)
+        readout(0, 3 * QUARTER)
+        cap_woven(3 * QUARTER)
+        finish(2 * QUARTER, 0)
         product(3)
-        finish(QUARTER, 1)
-        for pair in range(2):
-            finish(2 * QUARTER, pair)
+        finish(2 * QUARTER, 1)
         finish(3 * QUARTER, 0)
         finish(3 * QUARTER, 1, 2)

@@ -106,11 +106,6 @@ def tile_list_eclass_cost_extraction_kernel(
                 w4raw[b][:].bitcast(U16).rearrange("p (m t) -> p t m", t=4)[:, t0:t1, :],
             )
 
-        w2raw = {}
-
-        def load_w2(b):
-            w2raw[b] = placed([P, 4, N], F32, "w2raw%d" % b, LOW + 8192 * (1 - b))
-            nc.sync.dma_start(w2raw[b][:], w2[512 * b : 512 * (b + 1), :].rearrange("(p j) n -> p j n", j=4))
 
         vw_first = keep.tile([P, QUARTER], U32, name="vw_first", align_bytes=64)
         nc.vector.tensor_copy(vw_first[:], tabw[:].bitcast(U32).indirect(idx[:, 0:16]))
@@ -122,7 +117,6 @@ def tile_list_eclass_cost_extraction_kernel(
         nc.sync.dma_start(wgt_sb[:], wgt)
         gain_sb = placed([P, 2, 4], F32, "gain_sb", W4_LATE + 192)
         nc.sync.dma_start(gain_sb[:], gain.rearrange("(b p i) -> p b i", b=2, i=4))
-        load_w2(0)
         make_identity(nc, ident[:], nomemset=True)
         h = {}
 
@@ -164,7 +158,9 @@ def tile_list_eclass_cost_extraction_kernel(
                     part = late[:, BANK * d : BANK * (d + 1)]
                     nc.vector.tensor_copy(part, tabs[:].indirect(idx[:, 64 + 32 * d : 96 + 32 * d]))
                     carry(nc.sync, vs_late[:, BANK * (d + 1) : BANK * (d + 2)], part)
-                load_w2(1)
+                w2raw = placed([P, 2, 4, N], F32, "w2raw", LOW)
+                for b in range(2):
+                    nc.sync.dma_start(w2raw[:, b, :, :], w2[512 * b : 512 * (b + 1), :].rearrange("(p j) n -> p j n", j=4))
             if j > 0:
                 nc.vector.tensor_copy(codes, tabw[:].bitcast(U32).indirect(idx[:, lo // 16 : hi // 16]))
             for k in range(FIRST):
@@ -185,7 +181,7 @@ def tile_list_eclass_cost_extraction_kernel(
         for b in range(2):
             nc.vector.tensor_copy(
                 w2bf[:, b, :].rearrange("p (c i t) -> p c t i", i=4, t=4),
-                w2raw[b][:].rearrange("p t (c i) -> p c t i", i=4),
+                w2raw[:, b, :, :].rearrange("p t (c i) -> p c t i", i=4),
             )
         nc.vector.quantize_mx(out=w2w[:].bitcast(FP8X4), scales=w2s[:], in_=w2bf[:].rearrange("p b c -> p (b c)"))
 

from contextlib import ExitStack

import concourse.mybir as mybir
from concourse.masks import make_identity

K, T, S, M, H, N = 512, 4096, 2048, 1024, 1024, 512
FLOPS = 2 * K * H * S + 2 * H * N * M

F32 = mybir.dt.float32
BF16 = mybir.dt.bfloat16
I32 = mybir.dt.int32
U32 = mybir.dt.uint32
U16 = mybir.dt.uint16
U8 = mybir.dt.uint8
FP8X4 = mybir.dt.float8_e4m3fn_x4
FP4X4 = mybir.dt.float4_e2m1fn_x4
ALU = mybir.AluOpType
ACT = mybir.ActivationFunctionType

P = 128
BANK = 512
QUARTER = 256
CHUNKS = S // BANK
TILES = H // P
FIRST = 6
ROWS = P - 16
Y_BANK = ((0, 1), (2, 3), (4, 5), (6, 7))
TURNED = (0, QUARTER)


def tile_list_eclass_cost_extraction_kernel(
    tc, tab_words, tab_scales, offs, w4_words, w4_scales, gain, offs2, wgt, budget, w2, best, out
):
    nc = tc.nc
    with ExitStack() as ctx:
        keep = ctx.enter_context(tc.tile_pool(name="keep", bufs=1))
        psum = ctx.enter_context(tc.psum_pool(name="psum", bufs=1))
        head = ctx.enter_context(tc.tile_pool(name="head", bufs=1))
        mid = ctx.enter_context(tc.tile_pool(name="mid", bufs=1))

        def placed(shape, dtype, name, offset):
            return head.tile(shape, dtype, name=name, offset=offset, align_bytes=64)

        W4_LATE = 3008
        SPREAD0 = W4_LATE + H - 64
        SPREAD1 = SPREAD0 + BANK - 64
        VW_LATE = SPREAD1 + BANK - 64
        LATE = VW_LATE - 2 * BANK
        BUD_RAW = VW_LATE + 4096 + 128
        TABS = BUD_RAW + 16384 - 64
        LOW = TABS + T - 64
        HIGH = LOW + 16384

        tabs = placed([P, T], U8, "tabs", TABS)
        w4sraw = keep.tile([P, H], U8, name="w4sraw")
        idx = keep.tile([P, S // 16], U16, name="idx")
        nc.sync.dma_start(idx[:], offs)
        nc.scalar.dma_start(tabs[ROWS:P, :].bitcast(I32), tab_scales[0].bitcast(I32))
        nc.sync.dma_start(w4sraw[ROWS:P, :].bitcast(I32), w4_scales[0].bitcast(I32))
        tabw = keep.tile([P, T], I32, name="tabw", tag="tabw")
        words = tab_words[0].rearrange("p t i -> p (t i)").bitcast(I32)
        nc.sync.dma_start(tabw[:], words)
        w4raw = [placed([P, H], U8, "w4raw0", HIGH - H // 2)]
        nc.sync.dma_start(w4raw[0][:].bitcast(I32), w4_words[0, :, 0:H].bitcast(I32))
        idx2 = keep.tile([P, M // 16], U16, name="idx2")
        nc.sync.dma_start(idx2[:], offs2)
        nc.vector.memset(tabs[0:ROWS, :].bitcast(I32), 0)
        ident = keep.tile([P, P], F32, name="ident")
        nc.gpsimd.memset(ident[:], 0.0)
        SIGNS = 4 * M * TILES
        minus_one = {}
        for m0 in TURNED:
            minus_one[m0] = mid.tile([P, 1], F32, name="minus_one%d" % m0, offset=SIGNS + 4 * m0)
            nc.scalar.activation(minus_one[m0][:], ident[:, 0:1], ACT.Copy, scale=0.0, bias=-1.0)
        nc.gpsimd.memset(w4sraw[0:ROWS, :].bitcast(I32), 0)

        plane0 = keep.tile([P, BANK + H], U8, name="plane0", align_bytes=64)
        nc.gpsimd.memset(plane0[:].bitcast(I32), 0)
        vs_late = keep.tile([P, 3 * BANK], U8, name="vs_late", align_bytes=64)
        nc.gpsimd.memset(vs_late[:].bitcast(I32), 0)

        def carry(queue, plane, rows):
            for q in range(4):
                queue.dma_start(plane[32 * q : 32 * q + 4, :].bitcast(I32), rows[ROWS + 4 * q : ROWS + 4 * q + 4, :].bitcast(I32))

        stage0 = keep.tile([P, BANK + H], U8, name="stage0")
        for b in range(2):
            nc.vector.tensor_copy(
                stage0[:, BANK * (b + 1) : BANK * (b + 2)].rearrange("p (t m) -> p t m", t=4),
                w4sraw[:, BANK * b : BANK * (b + 1)].rearrange("p (m t) -> p t m", t=4),
            )
        spread0 = placed([P, BANK], U8, "spread0", SPREAD0)
        nc.vector.tensor_copy(spread0[:], tabs[:].indirect(idx[:, 0:32]))
        nc.vector.tensor_copy(stage0[96:P, 0:BANK].bitcast(I32), spread0[96:P, :].bitcast(I32))
        carry(nc.scalar, plane0[:], stage0[:])
        w4raw.append(placed([P, H], U8, "w4raw1", W4_LATE))
        nc.sync.dma_start(w4raw[1][:].bitcast(I32), w4_words[0, :, H : 2 * H].bitcast(I32))
        spread1 = placed([P, BANK], U8, "spread1", SPREAD1)
        nc.vector.tensor_copy(spread1[:], tabs[:].indirect(idx[:, 32:64]))
        carry(nc.sync, vs_late[:, 0:BANK], spread1[:])
        w4w = [keep.tile([P, H], U8, name="w4w%d" % b, align_bytes=64) for b in range(2)]

        def order_w4(b, t0, t1, move=nc.vector.tensor_copy):
            move(
                w4w[b][:].bitcast(U16).rearrange("p (t m) -> p t m", t=4)[:, t0:t1, :],
                w4raw[b][:].bitcast(U16).rearrange("p (m t) -> p t m", t=4)[:, t0:t1, :],
            )


        vw_first = keep.tile([P, QUARTER], U32, name="vw_first", align_bytes=64)
        nc.vector.tensor_copy(vw_first[:], tabw[:].bitcast(U32).indirect(idx[:, 0:16]))
        order_w4(0, 0, 2, nc.scalar.copy)
        order_w4(0, 2, 4, nc.scalar.copy)
        order_w4(1, 0, 4)
        vw_next = placed([P, QUARTER + BANK], U32, "vw_next", 0)
        wgt_sb = placed([P, M], F32, "wgt_sb", HIGH)
        nc.sync.dma_start(wgt_sb[:], wgt)
        gain_sb = placed([P, 2, 4], F32, "gain_sb", W4_LATE + 192)
        nc.sync.dma_start(gain_sb[:], gain.rearrange("(b p i) -> p b i", b=2, i=4))
        make_identity(nc, ident[:], nomemset=True)
        h = {}

        sums = []

        def bank(j, shape, name):
            return psum.tile(shape, F32, name=name, tag="bank%d" % j)

        def raw_cost(k, group):
            acc = bank(len(sums) % 8, [P, BANK], "acc")
            sums.append(acc)
            first, last = group[0][0], group[-1][1]
            for lo, hi, codes, scales in group:
                nc.tensor.matmul_mx(
                    out=acc[:, lo - first : hi - first],
                    lhsT=w4w[k // 4][:, 2 * P * (k % 4) : 2 * P * (k % 4 + 1)].bitcast(FP4X4),
                    lhsT_scale=plane0[:, BANK + P * k : BANK + P * (k + 1)],
                    rhs=codes.bitcast(FP8X4),
                    rhs_scale=scales,
                    start=True,
                    stop=True,
                )
            nc.scalar.activation(h[k][:, first:last], acc[:, 0 : last - first], ACT.Exp)

        for k in range(FIRST):
            h[k] = keep.tile([P, S], F32, name="h%d" % k, tag="h%d" % k)
        late = placed([P, 2 * BANK], U8, "late", LATE)
        vw_late = placed([P, 2 * BANK], U32, "vw_late", VW_LATE)
        runs = [
            (0, QUARTER, vw_first[:], plane0[:, 0:QUARTER]),
            (QUARTER, BANK, vw_next[:, 0:QUARTER], plane0[:, QUARTER:BANK]),
            (BANK, 2 * BANK, vw_next[:, QUARTER : QUARTER + BANK], vs_late[:, 0:BANK]),
            (2 * BANK, 3 * BANK, vw_late[:, 0:BANK], vs_late[:, BANK : 2 * BANK]),
            (3 * BANK, 4 * BANK, vw_late[:, BANK : 2 * BANK], vs_late[:, 2 * BANK : 3 * BANK]),
        ]
        for j, (lo, hi, codes, scales) in enumerate(runs):
            if j == 3:
                for d in range(2):
                    part = late[:, BANK * d : BANK * (d + 1)]
                    nc.vector.tensor_copy(part, tabs[:].indirect(idx[:, 64 + 32 * d : 96 + 32 * d]))
                    carry(nc.sync, vs_late[:, BANK * (d + 1) : BANK * (d + 2)], part)
                w2raw = placed([P, 2, 4, N], F32, "w2raw", LOW)
                for b in range(2):
                    nc.sync.dma_start(w2raw[:, b, :, :], w2[512 * b : 512 * (b + 1), :].rearrange("(p j) n -> p j n", j=4))
            if j > 0:
                nc.vector.tensor_copy(codes, tabw[:].bitcast(U32).indirect(idx[:, lo // 16 : hi // 16]))
            for k in range(FIRST):
                raw_cost(k, runs[j : j + 1])

        w2bf = keep.tile([P, 2, N * 4], BF16, name="w2bf", tag="w2bf", align_bytes=64)
        w2w = keep.tile([P, 2 * N], U32, name="w2w", align_bytes=64)
        w2s = keep.tile([P, 2 * N], U8, name="w2s", align_bytes=64)
        nc.gpsimd.memset(w2s[:, 0:N].bitcast(I32), 0)
        wg = {}
        for k in range(TILES):
            width = M
            for m0 in range(0, M, width):
                wg[k, m0] = mid.tile([P, width], F32, name="wg%d_%d" % (k, m0), offset=4 * M * k + 4 * m0)
                nc.vector.tensor_scalar(
                    wg[k, m0][:], wgt_sb[:, m0 : m0 + width], gain_sb[:, k // 4, k % 4 : k % 4 + 1], None, ALU.mult
                )
        for b in range(2):
            nc.vector.tensor_copy(
                w2bf[:, b, :].rearrange("p (c i t) -> p c t i", i=4, t=4),
                w2raw[:, b, :, :].rearrange("p t (c i) -> p c t i", i=4),
            )
        nc.vector.quantize_mx(out=w2w[:].bitcast(FP8X4), scales=w2s[:], in_=w2bf[:].rearrange("p b c -> p (b c)"))

        rows1 = budget[512:1024, :].rearrange("(p i) m -> p i m", i=4)
        bud_raw = placed([P, 2, 4, BANK], F32, "bud_raw", BUD_RAW)
        bud = {}
        bud_bf = keep.tile([P, 4 * M], BF16, name="bud_bf", tag="tabw")
        for half in range(2):
            nc.sync.dma_start(bud_raw[:, half, :, :], rows1[:, :, BANK * half : BANK * (half + 1)])
        for half in range(2):
            nc.vector.tensor_copy(
                bud_bf[:, 2 * M * half : 2 * M * (half + 1)].rearrange("p (c i t) -> p c t i", i=4, t=4),
                bud_raw[:, half, :, :].rearrange("p t (c i) -> p c t i", i=4),
            )
        best_t = {}

        def turn_best(m0, j):
            turn = bank(j, [P, 2, QUARTER], "turn")
            for mb in range(2):
                for nb in range(2):
                    nc.tensor.transpose(turn[:, mb, P * nb : P * (nb + 1)], res[m0, 1][:, nb, P * mb : P * (mb + 1)], ident[:])
            return turn

        bud[0] = placed([P, 4, M], F32, "bud0", HIGH + 4 * M - 64)
        nc.sync.dma_start(bud[0][:], budget[0:512, :].rearrange("(p i) m -> p i m", i=4))

        x = [placed([P, 4, M], F32, "x0", LOW - 16384), keep.tile([P, 4, M], F32, name="x1")]
        zw0 = keep.tile([P, M], U32, name="zw0", align_bytes=64)
        zs = [keep.tile([P, M], U8, name="zs%d" % b, align_bytes=64) for b in range(2)]
        zw = {(0, m0): zw0[:, m0 : m0 + QUARTER] for m0 in range(0, M, QUARTER)}
        z = {}

        def softplus(k):
            nc.scalar.activation(h[k][:], h[k][:], ACT.Ln, bias=1.0)

        def pick(k, m0, m1):
            nc.vector.tensor_tensor(
                x[k // 4][:, k % 4, m0:m1], h[k][:].indirect(idx2[:, m0 // 16 : m1 // 16]), wg[k, 0][:, m0:m1], ALU.mult
            )

        def cap_first_pass():
            z[0, 0] = mid.tile([P, 4 * M], BF16, name="z0", align_bytes=64, offset=4 * M * 3)
            nc.vector.tensor_tensor(
                z[0, 0][:].rearrange("p (c i t) -> p c t i", i=4, t=4),
                x[0][:].rearrange("p t (c i) -> p c t i", i=4),
                bud[0][:].rearrange("p t (c i) -> p c t i", i=4),
                ALU.min,
            )

        pairs = {}

        def round_pair(m0, u, move):
            if u == 0:
                pairs[m0] = mid.tile([P, 2, 2 * QUARTER], BF16, name="pairs%d" % m0, offset=8 * m0)
            move(
                pairs[m0][:, u, :].rearrange("p (c i t) -> p c t i", i=4, t=2),
                x[1][:, 2 * u : 2 * u + 2, m0 : m0 + QUARTER].rearrange("p t (c i) -> p c t i", i=4),
            )

        def cap_woven(m0):
            z[1, m0] = keep.tile([P, 4 * QUARTER], BF16, name="z1_%d" % m0, tag="z1_%d" % m0 if m0 < M - QUARTER else "minus_y0", align_bytes=64)
            nc.vector.tensor_tensor(
                z[1, m0][:].rearrange("p (c u t) -> p c u t", u=2, t=2),
                pairs[m0][:].rearrange("p u (c t) -> p c u t", t=2),
                bud_bf[:, 4 * m0 : 4 * (m0 + QUARTER)].rearrange("p (c u t) -> p c u t", u=2, t=2),
                ALU.min,
            )

        def quant(m0):
            offset = SIGNS + 4 * max(QUARTER, M - QUARTER - m0)
            zw[1, m0] = mid.tile([P, QUARTER], U32, name="zw1_%d" % m0, align_bytes=64, offset=offset)[:]
            nc.vector.quantize_mx(out=zw[1, m0].bitcast(FP8X4), scales=zs[1][:, m0 : m0 + QUARTER], in_=z[1, m0][:])

        y = {}

        def readout(b, m0, which=(0, 1)):
            for pair in which:
                if b == 0:
                    y[m0, pair] = bank(Y_BANK[m0 // QUARTER][pair], [P, 2, QUARTER], "y")
                if b == 0 and m0 in (QUARTER, BANK):
                    zplane = held[:, m0 - QUARTER : m0]
                else:
                    zplane = zs[b][:, m0 : m0 + QUARTER]
                for j in range(2):
                    if pair == 1 and m0 in TURNED:
                        moving = slice(N * b + QUARTER, N * (b + 1))
                        lhs, lhs_s, rhs, rhs_s = zw[b, m0][:, P * j : P * (j + 1)], zplane[:, P * j : P * (j + 1)], w2w[:, moving], w2s[:, moving]
                    else:
                        still = slice(N * b + P * (2 * pair + j), N * b + P * (2 * pair + j + 1))
                        lhs, lhs_s, rhs, rhs_s = w2w[:, still], w2s[:, still], zw[b, m0], zplane
                    nc.tensor.matmul_mx(
                        out=y[m0, pair][:, j, :],
                        lhsT=lhs.bitcast(FP8X4),
                        lhsT_scale=lhs_s,
                        rhs=rhs.bitcast(FP8X4),
                        rhs_scale=rhs_s,
                        start=(b == 0 and j == 0),
                        stop=(b == 1 and j == 1),
                    )

        res = {}

        def load_best(m0, pair, tile):
            res[m0, pair] = tile
            rows = best[2 * P * pair : 2 * P * (pair + 1), m0 : m0 + QUARTER]
            nc.sync.dma_start(tile, rows.rearrange("(t p) m -> p t m", p=P))

        def store(m0, pair, lo, hi, part, queue):
            rows = out[P * (2 * pair + lo) : P * (2 * pair + hi), m0 : m0 + QUARTER]
            queue.dma_start(rows.rearrange("(t p) m -> p t m", p=P), part)

        def finish(m0, pair, parts=1):
            for j in range(parts):
                lo, hi = 2 * j // parts, 2 * (j + 1) // parts
                part = res[m0, pair][:, lo:hi, :]
                nc.vector.tensor_tensor(part, y[m0, pair][:, lo:hi, :], part, ALU.subtract)
                store(m0, pair, lo, hi, part, nc.sync)

        minus_y = {}

        def leave_turned(m0):
            minus_y[m0] = keep.tile([P, 2, QUARTER], F32, name="minus_y%d" % m0, tag="minus_y%d" % m0, align_bytes=64)
            nc.scalar.activation(minus_y[m0][:], y[m0, 1][:], ACT.Copy, scale=minus_one[m0][:])

        back = {}

        def turn_back(m0, term, start, stop):
            for mb in range(2):
                for nb in range(2):
                    nc.tensor.matmul(
                        back[m0][:, nb, P * mb : P * (mb + 1)],
                        term[:, mb, P * nb : P * (nb + 1)],
                        ident[:],
                        start=start and (mb, nb) == (0, 0),
                        stop=stop and (mb, nb) == (1, 1),
                        is_transpose=True,
                    )

        def finish_turned(m0):
            turn_back(m0, minus_y[m0], False, True)
            res[m0, 1] = keep.tile([P, 2, QUARTER], F32, name="done%d" % m0)[:]
            nc.scalar.activation(res[m0, 1], back[m0][:], ACT.Copy, scale=-1.0)
            store(m0, 1, 0, 2, res[m0, 1], nc.scalar)

        for j in range(TILES):
            m0, pair = QUARTER * (j // 2), j % 2
            load_best(m0, pair, placed([P, 2, QUARTER], F32, "best%d" % j, LOW + 8 * QUARTER * j)[:])
        for k in range(FIRST):
            softplus(k)
            pick(k, 0, M)
            if k == 4:
                cap_first_pass()
        nc.vector.quantize_mx(out=zw0[:].bitcast(FP8X4), scales=zs[0][:], in_=z[0, 0][:])
        for m0 in range(0, M, QUARTER):
            round_pair(m0, 0, nc.vector.tensor_copy)
        for k in range(FIRST, TILES):
            h[k] = keep.tile([P, S], F32, name="h%d" % k, tag="h%d" % (k - FIRST))
            for group in (runs[0:2], runs[2:3], runs[3:4], runs[4:5]):
                raw_cost(k, group)
        readout(0, 0)
        turn = {m0: turn_best(m0, 6 + m0 // QUARTER) for m0 in TURNED}
        for k in range(FIRST, TILES - 1):
            softplus(k)
            pick(k, 0, M)
        last = TILES - 1
        softplus(last)

        held = mid.tile([P, BANK], U8, name="held", align_bytes=64, offset=4 * M * (TILES - 2))
        nc.scalar.copy(held[:].bitcast(U32), zs[0][:, QUARTER : M - QUARTER].bitcast(U32))

        def open_back(m0, tile):
            best_t[m0] = tile
            nc.scalar.copy(best_t[m0][:], turn[m0][:])
            back[m0] = bank(6 + m0 // QUARTER, [P, 2, QUARTER], "back")
            turn_back(m0, best_t[m0], True, False)

        readout(0, QUARTER)
        open_back(0, mid.tile([P, 2, QUARTER], F32, name="best_t0", offset=4 * M * (TILES - 2) + M))
        readout(0, 2 * QUARTER)

        def product(q, which=(0, 1)):
            quant(QUARTER * q)
            readout(1, QUARTER * q, which)

        for q in range(4):
            if q % 2 == 0:
                pick(last, QUARTER * q, QUARTER * (q + 2))
            round_pair(QUARTER * q, 1, nc.scalar.copy)
            if q == 1:
                open_back(QUARTER, keep.tile([P, 2, QUARTER], F32, name="best_t1", tag="h0"))
        cap_woven(0)
        cap_woven(QUARTER)
        product(0, (1, 0))
        product(1, (1, 0))
        cap_woven(2 * QUARTER)
        leave_turned(0)
        leave_turned(QUARTER)
        finish(0, 0)
        finish_turned(0)
        finish(QUARTER, 0)
        finish_turned(QUARTER)
        product(2)
        readout(0, 3 * QUARTER)
        cap_woven(3 * QUARTER)
        finish(2 * QUARTER, 0)
        product(3)
        finish(2 * QUARTER, 1)
        finish(3 * QUARTER, 0)
        finish(3 * QUARTER, 1, 2)
